import numpy as np
import ml_dtypes


def mxq(x, axis, fmt="e4m3"):
    dtype, down = {"e4m3": (ml_dtypes.float8_e4m3fn, 7), "e5m2": (ml_dtypes.float8_e5m2, 14)}[fmt]
    v = np.moveaxis(np.asarray(x, np.float32).astype(ml_dtypes.bfloat16).astype(np.float64), axis, -1)
    blocks = v.reshape(v.shape[:-1] + (-1, 32))
    amax = np.abs(blocks).max(-1, keepdims=True)
    byte = np.maximum(np.where(amax > 0, np.frexp(amax)[1] - 1 + 127, 0) - down, 1)
    scale = np.exp2(byte - 127.0)
    codes = (blocks / scale).astype(np.float32).astype(dtype).astype(np.float64)
    return np.moveaxis((codes * scale).reshape(v.shape), -1, axis)


WIDE = False


def mx_kscale(k):
    if not WIDE:
        return np.ones(k)
    levels = np.array([10, -10, 5, -5, 0])
    if k % 512:
        return np.exp2(np.random.permutation(np.resize(levels, k // 32))).repeat(32)
    a = np.empty((k // 512, 16))
    for p in range(k // 512):
        a[p, :8] = np.random.permutation(np.resize(levels, 8))
        for g in range(8):
            far = levels[np.abs(levels - a[p, g]) >= 10]
            a[p, g + 8] = far[np.random.randint(len(far))]
    return np.exp2(a.ravel()).repeat(32)


def f64(x):
    return np.asarray(x).astype(np.float64)


def striped(idx):
    return np.tile(idx.reshape(-1, 16).T, (8, 1)).astype(np.uint16)


def unstriped(offs):
    return offs[:16].T.reshape(-1).astype(np.int64)


E2M1 = np.array([0.0, 0.5, 1.0, 1.5, 2.0, 3.0, 4.0, 6.0, -0.0, -0.5, -1.0, -1.5, -2.0, -3.0, -4.0, -6.0])


def pack_weight(w, fmt):
    k, n = w.shape
    w = f64(np.asarray(w, np.float32).astype(ml_dtypes.bfloat16)).reshape(k // 32, 32, n)
    amax = np.abs(w).max(1)
    if fmt == "e4m3":
        byte = np.frexp(amax)[1] - 1 + 127 - 7
    else:
        mant, ex = np.frexp(amax / 6.0)
        byte = np.where(mant > 0.5, ex, ex - 1) + 127
    byte = np.clip(np.where(amax > 0, byte, 1), 1, 254)
    scaled = (w * np.exp2(127.0 - byte)[:, None, :]).reshape(k, n).astype(np.float32)
    by_word = np.ascontiguousarray(scaled.reshape(k // 512, 128, 4, n).transpose(0, 1, 3, 2))
    if fmt == "e4m3":
        words = by_word.astype(ml_dtypes.float8_e4m3fn).view(np.uint8)
    else:
        c = by_word.astype(ml_dtypes.float4_e2m1fn).view(np.uint8) & 0xF
        words = (c[..., 0::2] | (c[..., 1::2] << 4)).reshape(k // 512, 128, 2 * n)
    return np.ascontiguousarray(words), np.ascontiguousarray(byte.astype(np.uint8).reshape(k // 512, 16, n))


def unpack_weight(words, scales, fmt):
    g, _, n = scales.shape
    words = np.ascontiguousarray(words).reshape(g, 128, n, -1)
    if fmt == "e4m3":
        vals = words.view(ml_dtypes.float8_e4m3fn).astype(np.float64)
    else:
        nib = np.empty((g, 128, n, 4), np.uint8)
        nib[..., 0::2] = words & 0xF
        nib[..., 1::2] = words >> 4
        vals = E2M1[nib]
    vals = vals * np.repeat(np.exp2(scales.astype(np.float64) - 127.0), 8, axis=1)[..., None]
    return vals.transpose(0, 1, 3, 2).reshape(g * 512, n)


def gelu(v):
    return 0.5 * v * (1.0 + np.tanh(np.sqrt(2.0 / np.pi) * (v + 0.044715 * v**3)))


def bf(x):
    return np.asarray(x, np.float32).astype(ml_dtypes.bfloat16)


def planes(Y):
    n, m = Y.shape
    b = f64(bf(Y)).reshape(n // 32, 32, m)
    amax = np.abs(b).max(1)
    byte = np.clip(np.where(amax > 0, np.frexp(amax)[1] - 1 + 127 - 7, 1), 1, 254)
    codes = (b * np.exp2(127.0 - byte)[:, None, :]).reshape(n, m).astype(np.float32).astype(ml_dtypes.float8_e4m3fn).view(np.uint8)
    words = codes.reshape(n // 512, 128, 4, m).transpose(0, 1, 3, 2)
    return np.ascontiguousarray(words), np.ascontiguousarray(byte.astype(np.uint8).reshape(n // 512, 16, m))


K, K2, T, T3, S, H, T2, N = 1024, 512, 2048, 1024, 512, 1024, 1024, 512

def setup_inputs():
    n = np.random.standard_normal
    s, s2, u = mx_kscale(K)[:, None], mx_kscale(K2)[:, None], mx_kscale(H)[:, None]
    rg = np.exp(0.8 * n(N))
    tab_words, tab_scales = pack_weight(n((K, T)) * s, "e4m3")
    tab2_words, tab2_scales = pack_weight(n((K2, T3)) * s2, "e4m3")
    w1_words, w1_scales = pack_weight(n((K, H)) / np.sqrt(K) / s * u.T, "e2m1")
    wb_words, wb_scales = pack_weight(0.55 * n((K2, H)) / np.sqrt(K2) / s2, "e4m3")
    return {
        "tab_words": tab_words, "tab_scales": tab_scales,
        "tab2_words": tab2_words, "tab2_scales": tab2_scales,
        "offs": striped(np.random.permutation(T)[:S]),
        "offs2": striped(np.random.permutation(T3)[:S]),
        "offs3": striped(np.random.permutation(T2)[:S]),
        "offs4": striped(np.random.permutation(T2)[:S]),
        "w1_words": w1_words, "w1_scales": w1_scales,
        "wa": (1.6 * n((K2, H)) / np.sqrt(K2) / s2).astype(np.float32),
        "wb_words": wb_words, "wb_scales": wb_scales,
        "gain": (1.6 * np.exp(0.2 * n(H)) * u[:, 0]).astype(np.float32),
        "wg1": np.exp(0.3 * n((128, S))).astype(np.float32),
        "wg2": np.exp(0.3 * n((128, S))).astype(np.float32),
        "surf": (0.7 * n((H, T2)) * u).astype(np.float32),
        "wz": (0.6 * n((H, N)) / np.sqrt(H) / u * rg).astype(np.float32),
        "resid": (0.5 * n((N, T2)) * rg[:, None]).astype(np.float32),
    }

def reference(tab_words, tab_scales, tab2_words, tab2_scales, offs, offs2, offs3, offs4, w1_words, w1_scales, wa, wb_words, wb_scales, gain, wg1, wg2, surf, wz, resid):
    v = unpack_weight(tab_words, tab_scales, "e4m3")[:, unstriped(offs)]
    v2 = unpack_weight(tab2_words, tab2_scales, "e4m3")[:, unstriped(offs2)]
    h1 = unpack_weight(w1_words, w1_scales, "e2m1").T @ v
    ta = np.tanh(mxq(f64(wa), 0, "e4m3").T @ v2)
    tb = np.cos(unpack_weight(wb_words, wb_scales, "e4m3").T @ v2)
    h2 = (ta + tb) * f64(gain)[:, None]
    pa = np.zeros((H, T2))
    pa[:, unstriped(offs3)] = np.tile(f64(wg1), (H // 128, 1)) * h1
    pb = np.zeros((H, T2))
    pb[:, unstriped(offs4)] = np.tile(f64(wg2), (H // 128, 1)) * h2
    q = pa + f64(surf)
    z = np.maximum(q, pb) + q
    y = (mxq(f64(wz), 0, "e4m3").T @ mxq(z, 0, "e4m3")) + f64(resid)
    words, scales = planes(y)
    return y, words, scales

@@ -1,0 +1,340 @@
+import math
+from contextlib import ExitStack
+
+import concourse.mybir as mybir
+from concourse.masks import make_identity
+
+K, K2, T, T3, S, H, T2, N = 1024, 512, 2048, 1024, 512, 1024, 1024, 512
+FLOPS = 2 * S * H * (K + 2 * K2) + 2 * H * N * T2
+
+F32 = mybir.dt.float32
+BF16 = mybir.dt.bfloat16
+I32 = mybir.dt.int32
+U32 = mybir.dt.uint32
+U16 = mybir.dt.uint16
+U8 = mybir.dt.uint8
+E4M3 = mybir.dt.float8_e4m3fn_x4
+E2M1 = mybir.dt.float4_e2m1fn_x4
+ALU = mybir.AluOpType
+ACT = mybir.ActivationFunctionType
+
+P = 128
+SLICES = H // P
+GROUPS = H // 512
+ROUNDER = 1.5 * 2.0**23
+ECHO_PAGES = 3
+SEA_PAGES = 1
+WA_PART = 256
+CHUNK = 256
+CHUNKS = T2 // CHUNK
+
+
+def tile_list_altimeter_height_features_kernel(
+    tc, tab_words, tab_scales, tab2_words, tab2_scales, offs, offs2, offs3, offs4,
+    w1_words, w1_scales, wa, wb_words, wb_scales, gain, wg1, wg2, surf, wz, resid,
+    out_0, out_1, out_2,
+):
+    nc = tc.nc
+    with ExitStack() as ctx:
+        lists = ctx.enter_context(tc.tile_pool(name="lists", bufs=1))
+        keep = ctx.enter_context(tc.tile_pool(name="keep", bufs=1))
+        work = ctx.enter_context(tc.tile_pool(name="work", bufs=2))
+        psum = ctx.enter_context(tc.psum_pool(name="psum", bufs=1))
+
+        def load_list(src, name):
+            tile = lists.tile([P, S // 16], U16, name=name)
+            nc.sync.dma_start(tile[:], src)
+            return tile
+
+        def load_words(src, width, name):
+            tile = keep.tile([P, width], I32, name=name, align_bytes=64)
+            nc.sync.dma_start(tile[:], src.bitcast(I32))
+            return tile
+
+        def zeroed_scale_tile(engine, passes, width, name):
+            tile = keep.tile([P, passes, width // 4], I32, name=name, align_bytes=64)
+            engine.memset(tile[:], 0)
+            return tile
+
+        def load_scale_rows(queue, tile, src):
+            rows = src.bitcast(I32).rearrange("a q c -> q a c")
+            for quad in range(4):
+                queue.dma_start(tile[32 * quad : 32 * quad + 4], rows[4 * quad : 4 * quad + 4])
+
+        def gather(window, offsets, dtype, name):
+            picked = keep.tile([P, S], dtype, name=name, align_bytes=64)
+            nc.vector.tensor_copy(picked[:], window.bitcast(dtype).indirect(offsets[:]))
+            return picked
+
+        tab_sc = zeroed_scale_tile(nc.vector, 2, T, "tab_sc")
+        w1_sc = zeroed_scale_tile(nc.vector, 2, H, "w1_sc")
+        tab2_sc = zeroed_scale_tile(nc.gpsimd, 1, T3, "tab2_sc")
+        wb_sc = zeroed_scale_tile(nc.gpsimd, 1, H, "wb_sc")
+
+        load_scale_rows(nc.gpsimd, tab2_sc, tab2_scales)
+        load_scale_rows(nc.gpsimd, wb_sc, wb_scales)
+        idx = load_list(offs, "idx")
+        tab_w = [load_words(tab_words[0].rearrange("p t i -> p (t i)"), T, "tab_w0")]
+        load_scale_rows(nc.sync, tab_sc, tab_scales)
+        tab_w.append(load_words(tab_words[1].rearrange("p t i -> p (t i)"), T, "tab_w1"))
+        w1_w = keep.tile([P, 2, H // 2], I32, align_bytes=64)
+        nc.sync.dma_start(w1_w[:], w1_words.bitcast(I32).rearrange("a p c -> p a c"))
+        load_scale_rows(nc.sync, w1_sc, w1_scales)
+        idx2 = load_list(offs2, "idx2")
+        tab2_w = load_words(tab2_words[0].rearrange("p t i -> p (t i)"), T3, "tab2_w")
+        idx3 = load_list(offs3, "idx3")
+        wg1_sb = keep.tile([P, S], F32)
+        nc.sync.dma_start(wg1_sb[:], wg1)
+
+        def zeroed_page(engine, name):
+            page = keep.tile([P, T2], F32, name=name)
+            engine.memset(page[:], 0.0)
+            return page
+
+        ident = keep.tile([P, P], F32)
+        make_identity(nc, ident[:])
+        echo_pages = [zeroed_page(nc.vector if i < 2 else nc.gpsimd, "echo_page%d" % i) for i in range(ECHO_PAGES)]
+        sea_pages = [zeroed_page(nc.gpsimd, "sea_page%d" % i) for i in range(SEA_PAGES)]
+
+        surf_sb = {}
+
+        def load_surf(s):
+            tile = work.tile([P, T2], F32, name="surf_rows", bufs=ECHO_PAGES + 1)
+            nc.sync.dma_start(tile[:], surf[s * P : (s + 1) * P, :])
+            surf_sb[s] = tile
+
+        wa_raw = []
+
+        def load_wa(part):
+            raw = work.tile([P, 4, WA_PART], F32, name="wa_raw")
+            nc.sync.dma_start(raw[:], wa[:, WA_PART * part : WA_PART * (part + 1)].rearrange("(p j) c -> p j c", j=4))
+            wa_raw.append(raw)
+
+        load_wa(0)
+        wb_w = load_words(wb_words[0].rearrange("p c i -> p (c i)"), H, "wb_w")
+        idx4 = load_list(offs4, "idx4")
+        gain_sb = keep.tile([P, SLICES], F32)
+        with nc.allow_non_contiguous_dma(reason="one gain for each partition and slice"):
+            nc.sync.dma_start(gain_sb[:], gain.rearrange("(s p) -> p s", p=P))
+        wg2_sb = keep.tile([P, S], F32)
+        nc.sync.dma_start(wg2_sb[:], wg2)
+        load_surf(0)
+        load_wa(1)
+        load_surf(1)
+
+        v_w = [gather(tab_w[0][:], idx, U32, "v_w0")]
+        v_sc = [gather(tab_sc[:, a, :], idx, U8, "v_sc%d" % a) for a in range(2)]
+        v_w.append(gather(tab_w[1][:], idx, U32, "v_w1"))
+        v2_w = gather(tab2_w[:], idx2, U32, "v2_w")
+        v2_sc = gather(tab2_sc[:, 0, :], idx2, U8, "v2_sc")
+
+        wa_w = keep.tile([P, H], U32, align_bytes=64)
+        wa_sc = keep.tile([P, H], U8, align_bytes=64)
+        echo_acc, cos_acc, tanh_acc, rest_sb, tanh_sb, both_sb, doubled = {}, {}, {}, {}, {}, {}, {}
+
+        def sea_product(s, words, scales, name):
+            cols = slice(s * P, (s + 1) * P)
+            acc = psum.tile([P, S], F32, name=name)
+            nc.tensor.matmul_mx(out=acc[:], lhsT=words[:, cols].bitcast(E4M3), lhsT_scale=scales[:, cols],
+                                rhs=v2_w[:].bitcast(E4M3), rhs_scale=v2_sc[:], start=True, stop=True)
+            return acc
+
+        def echo_product(s, bank="echo_acc"):
+            acc = psum.tile([P, S], F32, name="echo_acc", tag=bank)
+            for a in range(2):
+                nc.tensor.matmul_mx(
+                    out=acc[:], lhsT=w1_w[:, a, :].bitcast(U8)[:, 2 * s * P : 2 * (s + 1) * P].bitcast(E2M1),
+                    lhsT_scale=w1_sc[:, a, :].bitcast(U8)[:, s * P : (s + 1) * P],
+                    rhs=v_w[a][:].bitcast(E4M3), rhs_scale=v_sc[a][:], start=(a == 0), stop=(a == 1))
+            echo_acc[s] = acc
+
+        def cos_product(s):
+            cos_acc[s] = sea_product(s, wb_w, wb_sc[:, 0, :].bitcast(U8), "cos_acc")
+
+        def tanh_product(s):
+            tanh_acc[s] = sea_product(s, wa_w, wa_sc, "tanh_acc")
+
+        def reduce_angle(s):
+            turns = work.tile([P, S], F32)
+            nc.scalar.activation(turns[:], cos_acc[s][:], ACT.Copy, bias=0.25, scale=1.0 / (2.0 * math.pi))
+            rest = work.tile([P, S], F32)
+            nc.scalar.activation(rest[:], turns[:], ACT.Copy, bias=ROUNDER, scale=1.0)
+            nc.vector.scalar_tensor_tensor(rest[:], rest[:], ROUNDER, turns[:], ALU.subtract, ALU.subtract)
+            rest_sb[s] = rest
+
+        def take_tanh(s):
+            tanh_sb[s] = work.tile([P, S], F32, name="tanh_sb")
+            nc.scalar.activation(tanh_sb[s][:], tanh_acc[s][:], ACT.Tanh)
+
+        def add_cos(s):
+            both = work.tile([P, S], F32)
+            nc.scalar.activation(both[:], rest_sb[s][:], ACT.Sin, scale=-2.0 * math.pi)
+            nc.vector.tensor_tensor(both[:], both[:], tanh_sb[s][:], ALU.add)
+            both_sb[s] = both
+
+        def place_sea(s):
+            weight = work.tile([P, S], F32)
+            nc.scalar.activation(weight[:], wg2_sb[:], ACT.Copy, scale=gain_sb[:, s : s + 1])
+            nc.vector.tensor_tensor(sea_pages[s % SEA_PAGES][:].indirect(idx4[:]), both_sb[s][:], weight[:], ALU.mult)
+
+        def place_echo(s):
+            h1 = work.tile([P, S], F32)
+            nc.scalar.copy(h1[:], echo_acc[s][:])
+            nc.vector.tensor_tensor(echo_pages[s % ECHO_PAGES][:].indirect(idx3[:]), h1[:], wg1_sb[:], ALU.mult)
+
+        def turned_sum(acc, parts, half):
+            for n, part in enumerate(parts):
+                for i in range(4):
+                    cols = slice((4 * half + i) * P, (4 * half + i + 1) * P)
+                    nc.tensor.matmul(acc[:, i * P : (i + 1) * P], lhsT=part[:, cols], rhs=ident[:],
+                                     start=(n == 0 and i == 0), stop=(n == len(parts) - 1 and i == 3),
+                                     is_transpose=True)
+
+        def by_word(acc):
+            return acc[:].rearrange("m (i p u e) -> m u i p e", i=4, u=2, e=2)
+
+        def double_q(s):
+            for half in range(2):
+                q_acc = psum.tile([P, 512], F32, name="q_acc", bufs=2)
+                turned_sum(q_acc, [surf_sb[s], echo_pages[s % ECHO_PAGES]], half)
+                twice = work.tile([P, 2, 4, 32, 2], F32, name="twice_q", bufs=6)
+                nc.scalar.activation(twice[:], by_word(q_acc), ACT.Copy, scale=2.0)
+                doubled[s, half] = twice
+
+        def quantise_wa(part):
+            cols = slice(WA_PART * part, WA_PART * (part + 1))
+            rounded = work.tile([P, WA_PART, 4], BF16, name="rounded", align_bytes=64)
+            nc.scalar.copy(rounded[:].rearrange("p (c i) j -> p c j i", i=4),
+                           wa_raw[part][:].rearrange("p j (c i) -> p c j i", i=4))
+            nc.vector.quantize_mx(out=wa_w[:, cols].bitcast(E4M3), scales=wa_sc[:, cols],
+                                  in_=rounded[:].rearrange("p c j -> p (c j)"))
+
+        z_turned = {}
+
+        def combine(s):
+            g, part = divmod(s, 4)
+            for half in range(2):
+                if part == 0:
+                    z_turned[g, half] = work.tile([P, 4, 2, 4, 64], BF16, name="z_turned%d" % half)
+                acc = psum.tile([P, 512], F32, name="sum_acc", bufs=2)
+                turned_sum(acc, [surf_sb[s], echo_pages[s % ECHO_PAGES], sea_pages[s % SEA_PAGES]], half)
+                dst = z_turned[g, half][:, :, :, part, :].rearrange("m i u (p e) -> m u i p e", e=2)
+                nc.vector.tensor_tensor(dst, by_word(acc), doubled[s, half][:], ALU.max)
+
+        z_w = [keep.tile([P, T2], U32, name="z_w%d" % g, align_bytes=64) for g in range(GROUPS)]
+        z_sc = [keep.tile([P, T2], U8, name="z_sc%d" % g, align_bytes=64) for g in range(GROUPS)]
+
+        def quantise_z(g, c, tag):
+            words = z_turned[g, c // 2][:].rearrange("m i u s x -> m (i u s x)").bitcast(F32)
+            acc = psum.tile([P, 512], F32, name="back_acc", tag=tag)
+            for i in range(2):
+                for u in range(2):
+                    block = 2 * (2 * (c % 2) + i) + u
+                    nc.tensor.transpose(acc[:, u * CHUNK + i * P : u * CHUNK + (i + 1) * P],
+                                        words[:, block * P : (block + 1) * P], ident[:])
+            z_in = work.tile([P, CHUNK, 2], F32, name="z_in", bufs=3, align_bytes=64)
+            nc.scalar.copy(z_in[:], acc[:].rearrange("p (u m) -> p m u", u=2))
+            cols = slice(c * CHUNK, (c + 1) * CHUNK)
+            nc.vector.quantize_mx(out=z_w[g][:, cols].bitcast(E4M3), scales=z_sc[g][:, cols],
+                                  in_=z_in[:].rearrange("p m u -> p (m u)").bitcast(BF16))
+
+        wz_w = keep.tile([P, GROUPS, N], U32, align_bytes=64)
+        wz_sc = keep.tile([P, GROUPS, N], U8, align_bytes=64)
+
+        def quantise_wz(g):
+            raw = work.tile([P, 4, N], F32, name="raw")
+            nc.sync.dma_start(raw[:], wz[512 * g : 512 * (g + 1), :].rearrange("(p j) n -> p j n", j=4))
+            rounded = work.tile([P, 512, 4], BF16, name="rounded", align_bytes=64)
+            nc.scalar.copy(rounded[:].rearrange("p (t q) j -> p q t j", t=4),
+                           raw[:].rearrange("p j (q t) -> p q t j", t=4))
+            nc.vector.quantize_mx(out=wz_w[:, g, :].bitcast(E4M3), scales=wz_sc[:, g, :],
+                                  in_=rounded[:].rearrange("p c j -> p (c j)"))
+
+        y_sb = []
+        resid_rows = resid.rearrange("(p t) m -> p t m", t=4)
+
+        echo_product(0)
+        place_echo(0)
+        cos_product(0)
+        reduce_angle(0)
+        quantise_wa(0)
+        tanh_product(0)
+        take_tanh(0)
+        echo_product(1, "cos_acc")
+        place_echo(1)
+        add_cos(0)
+        cos_product(1)
+        reduce_angle(1)
+        tanh_product(1)
+        take_tanh(1)
+        echo_product(2, "tanh_acc")
+        quantise_wa(1)
+        double_q(0)
+        for s in range(SLICES):
+            place_sea(s)
+            if s + 2 < SLICES:
+                load_surf(s + 2)
+                place_echo(s + 2)
+            if s == 0:
+                cos_product(2)
+                tanh_product(2)
+            combine(s)
+            if s + 1 < SLICES:
+                add_cos(s + 1)
+                double_q(s + 1)
+            if s + 2 < SLICES:
+                reduce_angle(s + 2)
+                take_tanh(s + 2)
+            if s in (1, 3):
+                load_wa(2 + s // 2)
+                quantise_wa(2 + s // 2)
+            if s + 3 < SLICES:
+                echo_product(s + 3)
+                cos_product(s + 3)
+                tanh_product(s + 3)
+            if s in (2, 3):
+                quantise_wz(s - 2)
+            if s == 3:
+                for c in range(CHUNKS):
+                    tile = keep.tile([P, 4, CHUNK], F32, name="y%d" % c)
+                    nc.sync.dma_start(tile[:], resid_rows[:, :, c * CHUNK : (c + 1) * CHUNK])
+                    y_sb.append(tile)
+            if s in (4, 5):
+                for c in range(2):
+                    quantise_z(0, 2 * (s - 4) + c, "back_acc")
+
+        y_w = keep.tile([P, T2], U32, align_bytes=64)
+        y_sc = keep.tile([P, T2], U8, align_bytes=64)
+        out_rows = out_0.rearrange("(p t) m -> p t m", t=4)
+        out_words = out_1[0].rearrange("p m t -> p (m t)").bitcast(I32)
+        out_scales = out_2[0].bitcast(I32)
+
+        for c in range(CHUNKS):
+            quantise_z(1, c, ("back_acc", "echo_acc")[c % 2])
+        for c in range(CHUNKS):
+            cols = slice(c * CHUNK, (c + 1) * CHUNK)
+            for pair in range(2):
+                if c % 2 == 0:
+                    acc = psum.tile([P, 512], F32, name="y_acc", tag=("cos_acc", "tanh_acc")[pair])
+                else:
+                    acc = psum.tile([P, 512], F32, name="y_acc", tag="q_acc", bufs=2)
+                for g in range(GROUPS):
+                    for e in range(2):
+                        t = 2 * pair + e
+                        nc.tensor.matmul_mx(
+                            out=acc[:, e * CHUNK : (e + 1) * CHUNK],
+                            lhsT=wz_w[:, g, t * P : (t + 1) * P].bitcast(E4M3),
+                            lhsT_scale=wz_sc[:, g, t * P : (t + 1) * P],
+                            rhs=z_w[g][:, cols].bitcast(E4M3), rhs_scale=z_sc[g][:, cols],
+                            start=(g == 0 and e == 0), stop=(g == GROUPS - 1 and e == 1))
+                rows = y_sb[c][:, 2 * pair : 2 * pair + 2, :]
+                nc.vector.tensor_tensor(rows, acc[:].rearrange("p (e m) -> p e m", e=2), rows, ALU.add)
+            nc.sync.dma_start(out_rows[:, :, cols], y_sb[c][:])
+            y_in = work.tile([P, CHUNK, 4], BF16, name="y_in", align_bytes=64)
+            nc.scalar.copy(y_in[:].rearrange("p (c i) t -> p c t i", i=4),
+                           y_sb[c][:].rearrange("p t (c i) -> p c t i", i=4))
+            nc.vector.quantize_mx(out=y_w[:, cols].bitcast(E4M3), scales=y_sc[:, cols],
+                                  in_=y_in[:].rearrange("p m t -> p (m t)"))
+            nc.sync.dma_start(out_words[:, cols], y_w[:, cols].bitcast(I32))
+        for quad in range(4):
+            nc.sync.dma_start(out_scales[4 * quad : 4 * quad + 4, :], y_sc[32 * quad : 32 * quad + 4, :].bitcast(I32))

@@ -25,6 +25,8 @@ ROUNDER = 1.5 * 2.0**23
 ECHO_PAGES = 3
 SEA_PAGES = 1
 WA_PART = 256
+Y_BANKS = ("q_acc0", "q_acc1", "cos_acc", "tanh_acc", "sum_acc1", "echo_acc", "sum_acc0", "back_acc")
+BACK_BANKS = ("back_acc", "echo_acc", "sum_acc0", "back_acc")
 CHUNK = 256
 CHUNKS = T2 // CHUNK
 
@@ -66,13 +68,14 @@ def tile_list_altimeter_height_features_kernel(
             nc.vector.tensor_copy(picked[:], window.bitcast(dtype).indirect(offsets[:]))
             return picked
 
+        warm = keep.tile([P, 1], F32)
+        nc.vector.memset(warm[:], 0.0)
+        nc.scalar.activation(warm[:], warm[:], ACT.Silu)
         tab_sc = zeroed_scale_tile(nc.vector, 2, T, "tab_sc")
         w1_sc = zeroed_scale_tile(nc.vector, 2, H, "w1_sc")
-        tab2_sc = zeroed_scale_tile(nc.gpsimd, 1, T3, "tab2_sc")
-        wb_sc = zeroed_scale_tile(nc.gpsimd, 1, H, "wb_sc")
+        tab2_sc = zeroed_scale_tile(nc.vector, 1, T3, "tab2_sc")
+        wb_sc = zeroed_scale_tile(nc.vector, 1, H, "wb_sc")
 
-        load_scale_rows(nc.gpsimd, tab2_sc, tab2_scales)
-        load_scale_rows(nc.gpsimd, wb_sc, wb_scales)
         idx = load_list(offs, "idx")
         tab_w = [load_words(tab_words[0].rearrange("p t i -> p (t i)"), T, "tab_w0")]
         load_scale_rows(nc.sync, tab_sc, tab_scales)
@@ -82,6 +85,7 @@ def tile_list_altimeter_height_features_kernel(
         load_scale_rows(nc.sync, w1_sc, w1_scales)
         idx2 = load_list(offs2, "idx2")
         tab2_w = load_words(tab2_words[0].rearrange("p t i -> p (t i)"), T3, "tab2_w")
+        load_scale_rows(nc.sync, tab2_sc, tab2_scales)
         idx3 = load_list(offs3, "idx3")
         wg1_sb = keep.tile([P, S], F32)
         nc.sync.dma_start(wg1_sb[:], wg1)
@@ -93,8 +97,8 @@ def tile_list_altimeter_height_features_kernel(
 
         ident = keep.tile([P, P], F32)
         make_identity(nc, ident[:])
-        echo_pages = [zeroed_page(nc.vector if i < 2 else nc.gpsimd, "echo_page%d" % i) for i in range(ECHO_PAGES)]
-        sea_pages = [zeroed_page(nc.gpsimd, "sea_page%d" % i) for i in range(SEA_PAGES)]
+        echo_pages = [zeroed_page(nc.vector, "echo_page%d" % i) for i in range(ECHO_PAGES)]
+        sea_pages = [zeroed_page(nc.vector, "sea_page%d" % i) for i in range(SEA_PAGES)]
 
         surf_sb = {}
 
@@ -110,9 +114,10 @@ def tile_list_altimeter_height_features_kernel(
             nc.sync.dma_start(raw[:], wa[:, WA_PART * part : WA_PART * (part + 1)].rearrange("(p j) c -> p j c", j=4))
             wa_raw.append(raw)
 
-        load_wa(0)
         wb_w = load_words(wb_words[0].rearrange("p c i -> p (c i)"), H, "wb_w")
+        load_scale_rows(nc.sync, wb_sc, wb_scales)
         idx4 = load_list(offs4, "idx4")
+        load_wa(0)
         gain_sb = keep.tile([P, SLICES], F32)
         with nc.allow_non_contiguous_dma(reason="one gain for each partition and slice"):
             nc.sync.dma_start(gain_sb[:], gain.rearrange("(s p) -> p s", p=P))
@@ -130,7 +135,7 @@ def tile_list_altimeter_height_features_kernel(
 
         wa_w = keep.tile([P, H], U32, align_bytes=64)
         wa_sc = keep.tile([P, H], U8, align_bytes=64)
-        echo_acc, cos_acc, tanh_acc, rest_sb, tanh_sb, both_sb, doubled = {}, {}, {}, {}, {}, {}, {}
+        echo_acc, cos_acc, tanh_acc, rest_sb, tanh_sb, both_sb, q_acc, doubled = {}, {}, {}, {}, {}, {}, {}, {}
 
         def sea_product(s, words, scales, name):
             cols = slice(s * P, (s + 1) * P)
@@ -139,8 +144,8 @@ def tile_list_altimeter_height_features_kernel(
                                 rhs=v2_w[:].bitcast(E4M3), rhs_scale=v2_sc[:], start=True, stop=True)
             return acc
 
-        def echo_product(s, bank="echo_acc"):
-            acc = psum.tile([P, S], F32, name="echo_acc", tag=bank)
+        def echo_product(s):
+            acc = psum.tile([P, S], F32, name="echo_acc")
             for a in range(2):
                 nc.tensor.matmul_mx(
                     out=acc[:], lhsT=w1_w[:, a, :].bitcast(U8)[:, 2 * s * P : 2 * (s + 1) * P].bitcast(E2M1),
@@ -155,9 +160,10 @@ def tile_list_altimeter_height_features_kernel(
             tanh_acc[s] = sea_product(s, wa_w, wa_sc, "tanh_acc")
 
         def reduce_angle(s):
-            turns = work.tile([P, S], F32)
+            tag, bufs = ("factor1", 1) if s == 0 else ("turns", 2)
+            turns = work.tile([P, S], F32, name="turns", tag=tag, bufs=bufs)
             nc.scalar.activation(turns[:], cos_acc[s][:], ACT.Copy, bias=0.25, scale=1.0 / (2.0 * math.pi))
-            rest = work.tile([P, S], F32)
+            rest = work.tile([P, S], F32, bufs=1)
             nc.scalar.activation(rest[:], turns[:], ACT.Copy, bias=ROUNDER, scale=1.0)
             nc.vector.scalar_tensor_tensor(rest[:], rest[:], ROUNDER, turns[:], ALU.subtract, ALU.subtract)
             rest_sb[s] = rest
@@ -167,39 +173,42 @@ def tile_list_altimeter_height_features_kernel(
             nc.scalar.activation(tanh_sb[s][:], tanh_acc[s][:], ACT.Tanh)
 
         def add_cos(s):
-            both = work.tile([P, S], F32)
+            both = work.tile([P, S], F32, name="both", tag="sea%d" % (s % 2), bufs=1)
             nc.scalar.activation(both[:], rest_sb[s][:], ACT.Sin, scale=-2.0 * math.pi)
             nc.vector.tensor_tensor(both[:], both[:], tanh_sb[s][:], ALU.add)
             both_sb[s] = both
 
         def place_sea(s):
-            weight = work.tile([P, S], F32)
+            weight = work.tile([P, S], F32, name="weight", tag="factor%d" % (s % 2), bufs=1)
             nc.scalar.activation(weight[:], wg2_sb[:], ACT.Copy, scale=gain_sb[:, s : s + 1])
             nc.vector.tensor_tensor(sea_pages[s % SEA_PAGES][:].indirect(idx4[:]), both_sb[s][:], weight[:], ALU.mult)
 
         def place_echo(s):
-            h1 = work.tile([P, S], F32)
+            h1 = work.tile([P, S], F32, name="h1", tag="factor%d" % (s % 2), bufs=1)
             nc.scalar.copy(h1[:], echo_acc[s][:])
             nc.vector.tensor_tensor(echo_pages[s % ECHO_PAGES][:].indirect(idx3[:]), h1[:], wg1_sb[:], ALU.mult)
 
-        def turned_sum(acc, parts, half):
+        def turned_sum(banks, parts):
             for n, part in enumerate(parts):
-                for i in range(4):
-                    cols = slice((4 * half + i) * P, (4 * half + i + 1) * P)
-                    nc.tensor.matmul(acc[:, i * P : (i + 1) * P], lhsT=part[:, cols], rhs=ident[:],
-                                     start=(n == 0 and i == 0), stop=(n == len(parts) - 1 and i == 3),
-                                     is_transpose=True)
+                for block in range(T2 // P):
+                    half, i = divmod(block, 4)
+                    nc.tensor.matmul(banks[half][:, i * P : (i + 1) * P], lhsT=part[:, block * P : (block + 1) * P],
+                                     rhs=ident[:], start=(n == 0 and i == 0),
+                                     stop=(n == len(parts) - 1 and i == 3), is_transpose=True)
 
         def by_word(acc):
             return acc[:].rearrange("m (i p u e) -> m u i p e", i=4, u=2, e=2)
 
+        def sum_q(s):
+            tags = ("cos_acc", "tanh_acc") if s == SLICES - 1 else ("q_acc0", "q_acc1")
+            q_acc[s] = [psum.tile([P, 512], F32, name="q_acc", tag=tag) for tag in tags]
+            turned_sum(q_acc[s], [surf_sb[s], echo_pages[s % ECHO_PAGES]])
+
         def double_q(s):
+            tag = ("sea%d" if s + 2 < SLICES else "twice_q%d") % (s % 2)
+            doubled[s] = work.tile([P, 2, 2, 4, 32, 2], F32, name="twice_q", tag=tag, bufs=1)
             for half in range(2):
-                q_acc = psum.tile([P, 512], F32, name="q_acc", bufs=2)
-                turned_sum(q_acc, [surf_sb[s], echo_pages[s % ECHO_PAGES]], half)
-                twice = work.tile([P, 2, 4, 32, 2], F32, name="twice_q", bufs=6)
-                nc.scalar.activation(twice[:], by_word(q_acc), ACT.Copy, scale=2.0)
-                doubled[s, half] = twice
+                nc.scalar.activation(doubled[s][:, half], by_word(q_acc[s][half]), ACT.Copy, scale=2.0)
 
         def quantise_wa(part):
             cols = slice(WA_PART * part, WA_PART * (part + 1))
@@ -213,13 +222,13 @@ def tile_list_altimeter_height_features_kernel(
 
         def combine(s):
             g, part = divmod(s, 4)
+            banks = [psum.tile([P, 512], F32, name="sum_acc%d" % half) for half in range(2)]
+            turned_sum(banks, [surf_sb[s], echo_pages[s % ECHO_PAGES], sea_pages[s % SEA_PAGES]])
             for half in range(2):
                 if part == 0:
                     z_turned[g, half] = work.tile([P, 4, 2, 4, 64], BF16, name="z_turned%d" % half)
-                acc = psum.tile([P, 512], F32, name="sum_acc", bufs=2)
-                turned_sum(acc, [surf_sb[s], echo_pages[s % ECHO_PAGES], sea_pages[s % SEA_PAGES]], half)
                 dst = z_turned[g, half][:, :, :, part, :].rearrange("m i u (p e) -> m u i p e", e=2)
-                nc.vector.tensor_tensor(dst, by_word(acc), doubled[s, half][:], ALU.max)
+                nc.vector.tensor_tensor(dst, by_word(banks[half]), doubled[s][:, half], ALU.max)
 
         z_w = [keep.tile([P, T2], U32, name="z_w%d" % g, align_bytes=64) for g in range(GROUPS)]
         z_sc = [keep.tile([P, T2], U8, name="z_sc%d" % g, align_bytes=64) for g in range(GROUPS)]
@@ -250,48 +259,69 @@ def tile_list_altimeter_height_features_kernel(
             nc.vector.quantize_mx(out=wz_w[:, g, :].bitcast(E4M3), scales=wz_sc[:, g, :],
                                   in_=rounded[:].rearrange("p c j -> p (c j)"))
 
+        y_acc = {}
+
+        def y_passes(c, pair, g):
+            cols = slice(c * CHUNK, (c + 1) * CHUNK)
+            for e in range(2):
+                t = 2 * pair + e
+                nc.tensor.matmul_mx(
+                    out=y_acc[c, pair][:, e * CHUNK : (e + 1) * CHUNK],
+                    lhsT=wz_w[:, g, t * P : (t + 1) * P].bitcast(E4M3), lhsT_scale=wz_sc[:, g, t * P : (t + 1) * P],
+                    rhs=z_w[g][:, cols].bitcast(E4M3), rhs_scale=z_sc[g][:, cols],
+                    start=(g == 0 and e == 0), stop=(g == GROUPS - 1 and e == 1))
+
+        def open_y(c):
+            for pair in range(2):
+                y_acc[c, pair] = psum.tile([P, 512], F32, name="y_acc", tag=Y_BANKS[2 * c + pair])
+                y_passes(c, pair, 0)
+
         y_sb = []
         resid_rows = resid.rearrange("(p t) m -> p t m", t=4)
 
         echo_product(0)
         place_echo(0)
+        echo_product(1)
         cos_product(0)
         reduce_angle(0)
         quantise_wa(0)
+        place_echo(1)
+        echo_product(2)
         tanh_product(0)
         take_tanh(0)
-        echo_product(1, "cos_acc")
-        place_echo(1)
         add_cos(0)
         cos_product(1)
         reduce_angle(1)
         tanh_product(1)
         take_tanh(1)
-        echo_product(2, "tanh_acc")
         quantise_wa(1)
-        double_q(0)
+        sum_q(0)
+        cos_product(2)
         for s in range(SLICES):
             place_sea(s)
-            if s + 2 < SLICES:
-                load_surf(s + 2)
-                place_echo(s + 2)
-            if s == 0:
-                cos_product(2)
-                tanh_product(2)
-            combine(s)
             if s + 1 < SLICES:
                 add_cos(s + 1)
-                double_q(s + 1)
             if s + 2 < SLICES:
                 reduce_angle(s + 2)
-                take_tanh(s + 2)
-            if s in (1, 3):
-                load_wa(2 + s // 2)
-                quantise_wa(2 + s // 2)
+                load_surf(s + 2)
+                place_echo(s + 2)
+                tanh_product(s + 2)
             if s + 3 < SLICES:
-                echo_product(s + 3)
                 cos_product(s + 3)
-                tanh_product(s + 3)
+                echo_product(s + 3)
+            double_q(s)
+            if s == SLICES - 2:
+                sum_q(s + 1)
+            if s == SLICES - 1:
+                open_y(1)
+            combine(s)
+            if s + 2 < SLICES:
+                sum_q(s + 1)
+            if s + 2 < SLICES:
+                take_tanh(s + 2)
+            if s in (0, 1):
+                load_wa(2 + s)
+                quantise_wa(2 + s)
             if s in (2, 3):
                 quantise_wz(s - 2)
             if s == 3:
@@ -299,9 +329,12 @@ def tile_list_altimeter_height_features_kernel(
                     tile = keep.tile([P, 4, CHUNK], F32, name="y%d" % c)
                     nc.sync.dma_start(tile[:], resid_rows[:, :, c * CHUNK : (c + 1) * CHUNK])
                     y_sb.append(tile)
-            if s in (4, 5):
-                for c in range(2):
-                    quantise_z(0, 2 * (s - 4) + c, "back_acc")
+            if s in (3, 4, 5):
+                quantise_z(0, s - 3, "back_acc")
+            if s == 5:
+                quantise_z(0, 3, "echo_acc")
+            if s == 6:
+                open_y(0)
 
         y_w = keep.tile([P, T2], U32, align_bytes=64)
         y_sc = keep.tile([P, T2], U8, align_bytes=64)
@@ -310,29 +343,19 @@ def tile_list_altimeter_height_features_kernel(
         out_scales = out_2[0].bitcast(I32)
 
         for c in range(CHUNKS):
-            quantise_z(1, c, ("back_acc", "echo_acc")[c % 2])
+            quantise_z(1, c, BACK_BANKS[c])
         for c in range(CHUNKS):
             cols = slice(c * CHUNK, (c + 1) * CHUNK)
+            if c >= 2:
+                open_y(c)
             for pair in range(2):
-                if c % 2 == 0:
-                    acc = psum.tile([P, 512], F32, name="y_acc", tag=("cos_acc", "tanh_acc")[pair])
-                else:
-                    acc = psum.tile([P, 512], F32, name="y_acc", tag="q_acc", bufs=2)
-                for g in range(GROUPS):
-                    for e in range(2):
-                        t = 2 * pair + e
-                        nc.tensor.matmul_mx(
-                            out=acc[:, e * CHUNK : (e + 1) * CHUNK],
-                            lhsT=wz_w[:, g, t * P : (t + 1) * P].bitcast(E4M3),
-                            lhsT_scale=wz_sc[:, g, t * P : (t + 1) * P],
-                            rhs=z_w[g][:, cols].bitcast(E4M3), rhs_scale=z_sc[g][:, cols],
-                            start=(g == 0 and e == 0), stop=(g == GROUPS - 1 and e == 1))
+                y_passes(c, pair, 1)
                 rows = y_sb[c][:, 2 * pair : 2 * pair + 2, :]
-                nc.vector.tensor_tensor(rows, acc[:].rearrange("p (e m) -> p e m", e=2), rows, ALU.add)
+                nc.vector.tensor_tensor(rows, y_acc[c, pair][:].rearrange("p (e m) -> p e m", e=2), rows, ALU.add)
             nc.sync.dma_start(out_rows[:, :, cols], y_sb[c][:])
             y_in = work.tile([P, CHUNK, 4], BF16, name="y_in", align_bytes=64)
-            nc.scalar.copy(y_in[:].rearrange("p (c i) t -> p c t i", i=4),
-                           y_sb[c][:].rearrange("p t (c i) -> p c t i", i=4))
+            rounding = nc.vector.tensor_copy if c == CHUNKS - 1 else nc.scalar.copy
+            rounding(y_in[:].rearrange("p (c i) t -> p c t i", i=4), y_sb[c][:].rearrange("p t (c i) -> p c t i", i=4))
             nc.vector.quantize_mx(out=y_w[:, cols].bitcast(E4M3), scales=y_sc[:, cols],
                                   in_=y_in[:].rearrange("p m t -> p (m t)"))
             nc.sync.dma_start(out_words[:, cols], y_w[:, cols].bitcast(I32))

@@ -23,10 +23,12 @@ SLICES = H // P
 GROUPS = H // 512
 ROUNDER = 1.5 * 2.0**23
 ECHO_PAGES = 3
-SEA_PAGES = 1
+SEA_PAGES = 2
 WA_PART = 256
-Y_BANKS = ("q_acc0", "q_acc1", "cos_acc", "tanh_acc", "sum_acc1", "echo_acc", "sum_acc0", "back_acc")
+Y_CHUNKS = ((0, 256), (256, 256), (512, 256), (768, 128), (896, 128))
+Y_BANKS = (("cos_acc", "tanh_acc"), ("q_acc0", "q_acc1"), ("sum_acc1", "echo_acc"), ("sum_acc0",), ("back_acc",))
 BACK_BANKS = ("back_acc", "echo_acc", "sum_acc0", "back_acc")
+EARLY_BACK = {3: ((0, "back_acc"),), 4: ((1, "back_acc"),), 5: ((2, "back_acc"), (3, "echo_acc"))}
 CHUNK = 256
 CHUNKS = T2 // CHUNK
 
@@ -79,6 +81,16 @@ def tile_list_altimeter_height_features_kernel(
         idx = load_list(offs, "idx")
         tab_w = [load_words(tab_words[0].rearrange("p t i -> p (t i)"), T, "tab_w0")]
         load_scale_rows(nc.sync, tab_sc, tab_scales)
+        gain_sb = keep.tile([P, SLICES], F32)
+        with nc.allow_non_contiguous_dma(reason="one gain for each partition and slice"):
+            nc.sync.dma_start(gain_sb[:], gain.rearrange("(s p) -> p s", p=P))
+        wg2_sb = keep.tile([P, S], F32)
+        nc.sync.dma_start(wg2_sb[:], wg2)
+        weights = []
+        for s in range(SLICES):
+            weight = work.tile([P, S], F32, name="weight", tag="factor%d" % s, bufs=1)
+            nc.scalar.activation(weight[:], wg2_sb[:], ACT.Copy, scale=gain_sb[:, s : s + 1])
+            weights.append(weight)
         tab_w.append(load_words(tab_words[1].rearrange("p t i -> p (t i)"), T, "tab_w1"))
         w1_w = keep.tile([P, 2, H // 2], I32, align_bytes=64)
         nc.sync.dma_start(w1_w[:], w1_words.bitcast(I32).rearrange("a p c -> p a c"))
@@ -98,7 +110,7 @@ def tile_list_altimeter_height_features_kernel(
         ident = keep.tile([P, P], F32)
         make_identity(nc, ident[:])
         echo_pages = [zeroed_page(nc.vector, "echo_page%d" % i) for i in range(ECHO_PAGES)]
-        sea_pages = [zeroed_page(nc.vector, "sea_page%d" % i) for i in range(SEA_PAGES)]
+        sea_pages = [zeroed_page(nc.gpsimd if i else nc.vector, "sea_page%d" % i) for i in range(SEA_PAGES)]
 
         surf_sb = {}
 
@@ -118,11 +130,6 @@ def tile_list_altimeter_height_features_kernel(
         load_scale_rows(nc.sync, wb_sc, wb_scales)
         idx4 = load_list(offs4, "idx4")
         load_wa(0)
-        gain_sb = keep.tile([P, SLICES], F32)
-        with nc.allow_non_contiguous_dma(reason="one gain for each partition and slice"):
-            nc.sync.dma_start(gain_sb[:], gain.rearrange("(s p) -> p s", p=P))
-        wg2_sb = keep.tile([P, S], F32)
-        nc.sync.dma_start(wg2_sb[:], wg2)
         load_surf(0)
         load_wa(1)
         load_surf(1)
@@ -160,7 +167,7 @@ def tile_list_altimeter_height_features_kernel(
             tanh_acc[s] = sea_product(s, wa_w, wa_sc, "tanh_acc")
 
         def reduce_angle(s):
-            tag, bufs = ("factor1", 1) if s == 0 else ("turns", 2)
+            tag, bufs = ("first1", 1) if s == 0 else ("turns", 2)
             turns = work.tile([P, S], F32, name="turns", tag=tag, bufs=bufs)
             nc.scalar.activation(turns[:], cos_acc[s][:], ACT.Copy, bias=0.25, scale=1.0 / (2.0 * math.pi))
             rest = work.tile([P, S], F32, bufs=1)
@@ -173,18 +180,17 @@ def tile_list_altimeter_height_features_kernel(
             nc.scalar.activation(tanh_sb[s][:], tanh_acc[s][:], ACT.Tanh)
 
         def add_cos(s):
-            both = work.tile([P, S], F32, name="both", tag="sea%d" % (s % 2), bufs=1)
+            tag = "sea%d" % (s % 2) if s < SLICES - 1 else "factor%d" % (s - 1)
+            both = work.tile([P, S], F32, name="both", tag=tag, bufs=1)
             nc.scalar.activation(both[:], rest_sb[s][:], ACT.Sin, scale=-2.0 * math.pi)
             nc.vector.tensor_tensor(both[:], both[:], tanh_sb[s][:], ALU.add)
             both_sb[s] = both
 
         def place_sea(s):
-            weight = work.tile([P, S], F32, name="weight", tag="factor%d" % (s % 2), bufs=1)
-            nc.scalar.activation(weight[:], wg2_sb[:], ACT.Copy, scale=gain_sb[:, s : s + 1])
-            nc.vector.tensor_tensor(sea_pages[s % SEA_PAGES][:].indirect(idx4[:]), both_sb[s][:], weight[:], ALU.mult)
+            nc.vector.tensor_tensor(sea_pages[s // (SLICES - 1)][:].indirect(idx4[:]), both_sb[s][:], weights[s][:], ALU.mult)
 
         def place_echo(s):
-            h1 = work.tile([P, S], F32, name="h1", tag="factor%d" % (s % 2), bufs=1)
+            h1 = work.tile([P, S], F32, name="h1", tag="factor%d" % (s - 2) if s >= 2 else "first%d" % s, bufs=1)
             nc.scalar.copy(h1[:], echo_acc[s][:])
             nc.vector.tensor_tensor(echo_pages[s % ECHO_PAGES][:].indirect(idx3[:]), h1[:], wg1_sb[:], ALU.mult)
 
@@ -200,13 +206,11 @@ def tile_list_altimeter_height_features_kernel(
             return acc[:].rearrange("m (i p u e) -> m u i p e", i=4, u=2, e=2)
 
         def sum_q(s):
-            tags = ("cos_acc", "tanh_acc") if s == SLICES - 1 else ("q_acc0", "q_acc1")
-            q_acc[s] = [psum.tile([P, 512], F32, name="q_acc", tag=tag) for tag in tags]
+            q_acc[s] = [psum.tile([P, 512], F32, name="q_acc%d" % half) for half in range(2)]
             turned_sum(q_acc[s], [surf_sb[s], echo_pages[s % ECHO_PAGES]])
 
         def double_q(s):
-            tag = ("sea%d" if s + 2 < SLICES else "twice_q%d") % (s % 2)
-            doubled[s] = work.tile([P, 2, 2, 4, 32, 2], F32, name="twice_q", tag=tag, bufs=1)
+            doubled[s] = work.tile([P, 2, 2, 4, 32, 2], BF16, name="twice_q", bufs=4)
             for half in range(2):
                 nc.scalar.activation(doubled[s][:, half], by_word(q_acc[s][half]), ACT.Copy, scale=2.0)
 
@@ -223,12 +227,18 @@ def tile_list_altimeter_height_features_kernel(
         def combine(s):
             g, part = divmod(s, 4)
             banks = [psum.tile([P, 512], F32, name="sum_acc%d" % half) for half in range(2)]
-            turned_sum(banks, [surf_sb[s], echo_pages[s % ECHO_PAGES], sea_pages[s % SEA_PAGES]])
+            turned_sum(banks, [surf_sb[s], echo_pages[s % ECHO_PAGES], sea_pages[s // (SLICES - 1)]])
+            if s < SLICES - 1:
+                rounded_sum = work.tile([P, 2, 2, 4, 32, 2], BF16, name="rounded_sum", tag="sea%d" % (s % 2), bufs=1)
             for half in range(2):
                 if part == 0:
                     z_turned[g, half] = work.tile([P, 4, 2, 4, 64], BF16, name="z_turned%d" % half)
                 dst = z_turned[g, half][:, :, :, part, :].rearrange("m i u (p e) -> m u i p e", e=2)
-                nc.vector.tensor_tensor(dst, by_word(banks[half]), doubled[s][:, half], ALU.max)
+                summed = by_word(banks[half])
+                if s < SLICES - 1:
+                    nc.scalar.copy(rounded_sum[:, half], summed)
+                    summed = rounded_sum[:, half]
+                nc.vector.tensor_tensor(dst, summed, doubled[s][:, half], ALU.max)
 
         z_w = [keep.tile([P, T2], U32, name="z_w%d" % g, align_bytes=64) for g in range(GROUPS)]
         z_sc = [keep.tile([P, T2], U8, name="z_sc%d" % g, align_bytes=64) for g in range(GROUPS)]
@@ -254,27 +264,31 @@ def tile_list_altimeter_height_features_kernel(
             raw = work.tile([P, 4, N], F32, name="raw")
             nc.sync.dma_start(raw[:], wz[512 * g : 512 * (g + 1), :].rearrange("(p j) n -> p j n", j=4))
             rounded = work.tile([P, 512, 4], BF16, name="rounded", align_bytes=64)
-            nc.scalar.copy(rounded[:].rearrange("p (t q) j -> p q t j", t=4),
-                           raw[:].rearrange("p j (q t) -> p q t j", t=4))
+            for half in range(2):
+                part = slice(64 * half, 64 * (half + 1))
+                nc.scalar.copy(rounded[:].rearrange("p (t q) j -> p q t j", t=4)[:, part],
+                               raw[:].rearrange("p j (q t) -> p q t j", t=4)[:, part])
             nc.vector.quantize_mx(out=wz_w[:, g, :].bitcast(E4M3), scales=wz_sc[:, g, :],
                                   in_=rounded[:].rearrange("p c j -> p (c j)"))
 
         y_acc = {}
 
-        def y_passes(c, pair, g):
-            cols = slice(c * CHUNK, (c + 1) * CHUNK)
-            for e in range(2):
-                t = 2 * pair + e
+        def y_passes(c, bank, g):
+            first, width = Y_CHUNKS[c]
+            cols = slice(first, first + width)
+            rows = 512 // width
+            for e in range(rows):
+                t = rows * bank + e
                 nc.tensor.matmul_mx(
-                    out=y_acc[c, pair][:, e * CHUNK : (e + 1) * CHUNK],
+                    out=y_acc[c][bank][:, e * width : (e + 1) * width],
                     lhsT=wz_w[:, g, t * P : (t + 1) * P].bitcast(E4M3), lhsT_scale=wz_sc[:, g, t * P : (t + 1) * P],
                     rhs=z_w[g][:, cols].bitcast(E4M3), rhs_scale=z_sc[g][:, cols],
-                    start=(g == 0 and e == 0), stop=(g == GROUPS - 1 and e == 1))
+                    start=(g == 0 and e == 0), stop=(g == GROUPS - 1 and e == rows - 1))
 
         def open_y(c):
-            for pair in range(2):
-                y_acc[c, pair] = psum.tile([P, 512], F32, name="y_acc", tag=Y_BANKS[2 * c + pair])
-                y_passes(c, pair, 0)
+            y_acc[c] = [psum.tile([P, 512], F32, name="y_acc", tag=tag) for tag in Y_BANKS[c]]
+            for bank in range(len(y_acc[c])):
+                y_passes(c, bank, 0)
 
         y_sb = []
         resid_rows = resid.rearrange("(p t) m -> p t m", t=4)
@@ -296,28 +310,29 @@ def tile_list_altimeter_height_features_kernel(
         take_tanh(1)
         quantise_wa(1)
         sum_q(0)
+        double_q(0)
+        sum_q(1)
         cos_product(2)
         for s in range(SLICES):
             place_sea(s)
+            if s + 2 < SLICES:
+                load_surf(s + 2)
+                place_echo(s + 2)
             if s + 1 < SLICES:
                 add_cos(s + 1)
             if s + 2 < SLICES:
                 reduce_angle(s + 2)
-                load_surf(s + 2)
-                place_echo(s + 2)
                 tanh_product(s + 2)
             if s + 3 < SLICES:
                 cos_product(s + 3)
                 echo_product(s + 3)
-            double_q(s)
-            if s == SLICES - 2:
-                sum_q(s + 1)
             if s == SLICES - 1:
                 open_y(1)
             combine(s)
+            if s + 1 < SLICES:
+                double_q(s + 1)
             if s + 2 < SLICES:
-                sum_q(s + 1)
-            if s + 2 < SLICES:
+                sum_q(s + 2)
                 take_tanh(s + 2)
             if s in (0, 1):
                 load_wa(2 + s)
@@ -325,14 +340,12 @@ def tile_list_altimeter_height_features_kernel(
             if s in (2, 3):
                 quantise_wz(s - 2)
             if s == 3:
-                for c in range(CHUNKS):
-                    tile = keep.tile([P, 4, CHUNK], F32, name="y%d" % c)
-                    nc.sync.dma_start(tile[:], resid_rows[:, :, c * CHUNK : (c + 1) * CHUNK])
+                for c, (first, width) in enumerate(Y_CHUNKS):
+                    tile = keep.tile([P, 4, width], F32, name="y%d" % c)
+                    nc.sync.dma_start(tile[:], resid_rows[:, :, first : first + width])
                     y_sb.append(tile)
-            if s in (3, 4, 5):
-                quantise_z(0, s - 3, "back_acc")
-            if s == 5:
-                quantise_z(0, 3, "echo_acc")
+            for c, tag in EARLY_BACK.get(s, ()):
+                quantise_z(0, c, tag)
             if s == 6:
                 open_y(0)
 
@@ -344,20 +357,24 @@ def tile_list_altimeter_height_features_kernel(
 
         for c in range(CHUNKS):
             quantise_z(1, c, BACK_BANKS[c])
-        for c in range(CHUNKS):
-            cols = slice(c * CHUNK, (c + 1) * CHUNK)
+        for c, (first, width) in enumerate(Y_CHUNKS):
+            cols = slice(first, first + width)
             if c >= 2:
                 open_y(c)
-            for pair in range(2):
-                y_passes(c, pair, 1)
-                rows = y_sb[c][:, 2 * pair : 2 * pair + 2, :]
-                nc.vector.tensor_tensor(rows, y_acc[c, pair][:].rearrange("p (e m) -> p e m", e=2), rows, ALU.add)
+            for bank, acc in enumerate(y_acc[c]):
+                y_passes(c, bank, 1)
+                count = 512 // width
+                rows = y_sb[c][:, count * bank : count * (bank + 1), :]
+                nc.vector.tensor_tensor(rows, acc[:].rearrange("p (e m) -> p e m", e=count), rows, ALU.add)
             nc.sync.dma_start(out_rows[:, :, cols], y_sb[c][:])
-            y_in = work.tile([P, CHUNK, 4], BF16, name="y_in", align_bytes=64)
-            rounding = nc.vector.tensor_copy if c == CHUNKS - 1 else nc.scalar.copy
+            y_in = work.tile([P, width, 4], BF16, name="y_in", bufs=3, align_bytes=64)
+            rounding = nc.vector.tensor_copy if c == len(Y_CHUNKS) - 1 else nc.scalar.copy
             rounding(y_in[:].rearrange("p (c i) t -> p c t i", i=4), y_sb[c][:].rearrange("p t (c i) -> p c t i", i=4))
             nc.vector.quantize_mx(out=y_w[:, cols].bitcast(E4M3), scales=y_sc[:, cols],
                                   in_=y_in[:].rearrange("p m t -> p (m t)"))
-            nc.sync.dma_start(out_words[:, cols], y_w[:, cols].bitcast(I32))
+            if first + width == T2 // 2:
+                nc.sync.dma_start(out_words[:, : T2 // 2], y_w[:, : T2 // 2].bitcast(I32))
+        nc.scalar.dma_start(out_words[:, T2 // 2 :], y_w[:, T2 // 2 :].bitcast(I32))
         for quad in range(4):
-            nc.sync.dma_start(out_scales[4 * quad : 4 * quad + 4, :], y_sc[32 * quad : 32 * quad + 4, :].bitcast(I32))
+            queue = nc.sync if quad < 2 else nc.scalar
+            queue.dma_start(out_scales[4 * quad : 4 * quad + 4, :], y_sc[32 * quad : 32 * quad + 4, :].bitcast(I32))

@@ -55,15 +55,15 @@ def tile_list_altimeter_height_features_kernel(
             nc.sync.dma_start(tile[:], src.bitcast(I32))
             return tile
 
-        def zeroed_scale_tile(engine, passes, width, name):
+        def zeroed_scale_tile(passes, width, name):
             tile = keep.tile([P, passes, width // 4], I32, name=name, align_bytes=64)
-            engine.memset(tile[:], 0)
+            nc.vector.memset(tile[:], 0)
             return tile
 
-        def load_scale_rows(queue, tile, src):
-            rows = src.bitcast(I32).rearrange("a q c -> q a c")
-            for quad in range(4):
-                queue.dma_start(tile[32 * quad : 32 * quad + 4], rows[4 * quad : 4 * quad + 4])
+        def load_scale_rows(tile, src):
+            rows = src.bitcast(I32).rearrange("a (q r) c -> r q a c", r=4)
+            for r in range(4):
+                nc.sync.dma_start(tile[r:P:32], rows[r])
 
         def gather(window, offsets, dtype, name):
             picked = keep.tile([P, S], dtype, name=name, align_bytes=64)
@@ -73,19 +73,25 @@ def tile_list_altimeter_height_features_kernel(
         warm = keep.tile([P, 1], F32)
         nc.vector.memset(warm[:], 0.0)
         nc.scalar.activation(warm[:], warm[:], ACT.Silu)
-        tab_sc = zeroed_scale_tile(nc.vector, 2, T, "tab_sc")
-        w1_sc = zeroed_scale_tile(nc.vector, 2, H, "w1_sc")
-        tab2_sc = zeroed_scale_tile(nc.vector, 1, T3, "tab2_sc")
-        wb_sc = zeroed_scale_tile(nc.vector, 1, H, "wb_sc")
+        tab_sc = zeroed_scale_tile(2, T, "tab_sc")
+        w1_sc = zeroed_scale_tile(2, H, "w1_sc")
+        tab2_sc = zeroed_scale_tile(1, T3, "tab2_sc")
+        wb_sc = zeroed_scale_tile(1, H, "wb_sc")
 
+        gain_rows = keep.tile([P, P], F32)
+        nc.gpsimd.memset(gain_rows[:], 0.0)
+        ident = keep.tile([P, P], F32)
+        make_identity(nc, ident[:])
         idx = load_list(offs, "idx")
         tab_w = [load_words(tab_words[0].rearrange("p t i -> p (t i)"), T, "tab_w0")]
-        load_scale_rows(nc.sync, tab_sc, tab_scales)
-        gain_sb = keep.tile([P, SLICES], F32)
-        with nc.allow_non_contiguous_dma(reason="one gain for each partition and slice"):
-            nc.sync.dma_start(gain_sb[:], gain.rearrange("(s p) -> p s", p=P))
+        load_scale_rows(tab_sc, tab_scales)
+        nc.sync.dma_start(gain_rows[:SLICES, :], gain.rearrange("(s p) -> s p", p=P))
         wg2_sb = keep.tile([P, S], F32)
         nc.sync.dma_start(wg2_sb[:], wg2)
+        gain_acc = psum.tile([P, 512], F32, name="gain_acc", tag="back_acc")
+        nc.tensor.transpose(gain_acc[:, :P], gain_rows[:], ident[:])
+        gain_sb = keep.tile([P, SLICES], F32)
+        nc.scalar.copy(gain_sb[:], gain_acc[:, :SLICES])
         weights = []
         for s in range(SLICES):
             weight = work.tile([P, S], F32, name="weight", tag="factor%d" % s, bufs=1)
@@ -94,23 +100,21 @@ def tile_list_altimeter_height_features_kernel(
         tab_w.append(load_words(tab_words[1].rearrange("p t i -> p (t i)"), T, "tab_w1"))
         w1_w = keep.tile([P, 2, H // 2], I32, align_bytes=64)
         nc.sync.dma_start(w1_w[:], w1_words.bitcast(I32).rearrange("a p c -> p a c"))
-        load_scale_rows(nc.sync, w1_sc, w1_scales)
+        load_scale_rows(w1_sc, w1_scales)
         idx2 = load_list(offs2, "idx2")
         tab2_w = load_words(tab2_words[0].rearrange("p t i -> p (t i)"), T3, "tab2_w")
-        load_scale_rows(nc.sync, tab2_sc, tab2_scales)
+        load_scale_rows(tab2_sc, tab2_scales)
         idx3 = load_list(offs3, "idx3")
         wg1_sb = keep.tile([P, S], F32)
         nc.sync.dma_start(wg1_sb[:], wg1)
 
-        def zeroed_page(engine, name):
+        def zeroed_page(name):
             page = keep.tile([P, T2], F32, name=name)
-            engine.memset(page[:], 0.0)
+            nc.gpsimd.memset(page[:], 0.0)
             return page
 
-        ident = keep.tile([P, P], F32)
-        make_identity(nc, ident[:])
-        echo_pages = [zeroed_page(nc.vector, "echo_page%d" % i) for i in range(ECHO_PAGES)]
-        sea_pages = [zeroed_page(nc.gpsimd if i else nc.vector, "sea_page%d" % i) for i in range(SEA_PAGES)]
+        echo_pages = [zeroed_page("echo_page%d" % i) for i in range(ECHO_PAGES)]
+        sea_pages = [zeroed_page("sea_page%d" % i) for i in range(SEA_PAGES)]
 
         surf_sb = {}
 
@@ -127,7 +131,7 @@ def tile_list_altimeter_height_features_kernel(
             wa_raw.append(raw)
 
         wb_w = load_words(wb_words[0].rearrange("p c i -> p (c i)"), H, "wb_w")
-        load_scale_rows(nc.sync, wb_sc, wb_scales)
+        load_scale_rows(wb_sc, wb_scales)
         idx4 = load_list(offs4, "idx4")
         load_wa(0)
         load_surf(0)
@@ -212,7 +216,7 @@ def tile_list_altimeter_height_features_kernel(
         def double_q(s):
             doubled[s] = work.tile([P, 2, 2, 4, 32, 2], BF16, name="twice_q", bufs=4)
             for half in range(2):
-                nc.scalar.activation(doubled[s][:, half], by_word(q_acc[s][half]), ACT.Copy, scale=2.0)
+                nc.scalar.activation(doubled[s][:, :, half], by_word(q_acc[s][half]), ACT.Copy, scale=2.0)
 
         def quantise_wa(part):
             cols = slice(WA_PART * part, WA_PART * (part + 1))
@@ -228,23 +232,23 @@ def tile_list_altimeter_height_features_kernel(
             g, part = divmod(s, 4)
             banks = [psum.tile([P, 512], F32, name="sum_acc%d" % half) for half in range(2)]
             turned_sum(banks, [surf_sb[s], echo_pages[s % ECHO_PAGES], sea_pages[s // (SLICES - 1)]])
+            if part == 0:
+                z_turned[g] = work.tile([P, 2, 4, 2, 4, 64], BF16, name="z_turned")
+            dst = z_turned[g][:, :, :, :, part, :].rearrange("m h i u (p e) -> m u h i p e", e=2)
             if s < SLICES - 1:
                 rounded_sum = work.tile([P, 2, 2, 4, 32, 2], BF16, name="rounded_sum", tag="sea%d" % (s % 2), bufs=1)
-            for half in range(2):
-                if part == 0:
-                    z_turned[g, half] = work.tile([P, 4, 2, 4, 64], BF16, name="z_turned%d" % half)
-                dst = z_turned[g, half][:, :, :, part, :].rearrange("m i u (p e) -> m u i p e", e=2)
-                summed = by_word(banks[half])
-                if s < SLICES - 1:
-                    nc.scalar.copy(rounded_sum[:, half], summed)
-                    summed = rounded_sum[:, half]
-                nc.vector.tensor_tensor(dst, summed, doubled[s][:, half], ALU.max)
+                for half in range(2):
+                    nc.scalar.copy(rounded_sum[:, :, half], by_word(banks[half]))
+                nc.vector.tensor_tensor(dst, rounded_sum[:], doubled[s][:], ALU.max)
+            else:
+                for half in range(2):
+                    nc.vector.tensor_tensor(dst[:, :, half], by_word(banks[half]), doubled[s][:, :, half], ALU.max)
 
         z_w = [keep.tile([P, T2], U32, name="z_w%d" % g, align_bytes=64) for g in range(GROUPS)]
         z_sc = [keep.tile([P, T2], U8, name="z_sc%d" % g, align_bytes=64) for g in range(GROUPS)]
 
         def quantise_z(g, c, tag):
-            words = z_turned[g, c // 2][:].rearrange("m i u s x -> m (i u s x)").bitcast(F32)
+            words = z_turned[g][:, c // 2].rearrange("m i u s x -> m (i u s x)").bitcast(F32)
             acc = psum.tile([P, 512], F32, name="back_acc", tag=tag)
             for i in range(2):
                 for u in range(2):

@@ -22,15 +22,19 @@ P = 128
 SLICES = H // P
 GROUPS = H // 512
 ROUNDER = 1.5 * 2.0**23
-ECHO_PAGES = 3
+GROUP_SLICES = SLICES // GROUPS
+AHEAD = 2
+ECHO_PAGES = AHEAD + 1
 SEA_PAGES = 2
-WA_PART = 256
-Y_CHUNKS = ((0, 256), (256, 256), (512, 256), (768, 128), (896, 128))
-Y_BANKS = (("cos_acc", "tanh_acc"), ("q_acc0", "q_acc1"), ("sum_acc1", "echo_acc"), ("sum_acc0",), ("back_acc",))
-BACK_BANKS = ("back_acc", "echo_acc", "sum_acc0", "back_acc")
-EARLY_BACK = {3: ((0, "back_acc"),), 4: ((1, "back_acc"),), 5: ((2, "back_acc"), (3, "echo_acc"))}
+WA_PART = 2 * P
+WA_PARTS = H // WA_PART
 CHUNK = 256
 CHUNKS = T2 // CHUNK
+BACK_PER_ROUND = 2
+Y_CHUNKS = ((0, 256), (256, 256), (512, 256), (768, 128), (896, 128))
+EARLY_BACK_BANKS = ("back_acc", "back_acc", "back_acc", "echo_acc")
+LATE_BACK_BANKS = ("back_acc", "echo_acc", "sum_acc0", "back_acc")
+Y_BANKS = (("cos_acc", "tanh_acc"), ("q_acc0", "q_acc1"), ("sum_acc1", "echo_acc"), ("sum_acc0",), ("back_acc",))
 
 
 def tile_list_altimeter_height_features_kernel(
@@ -61,9 +65,9 @@ def tile_list_altimeter_height_features_kernel(
             return tile
 
         def load_scale_rows(tile, src):
-            rows = src.bitcast(I32).rearrange("a (q r) c -> r q a c", r=4)
-            for r in range(4):
-                nc.sync.dma_start(tile[r:P:32], rows[r])
+            by_row = src.bitcast(I32).rearrange("a (d i) c -> i d a c", i=4)
+            for i in range(4):
+                nc.sync.dma_start(tile[i:P:32], by_row[i])
 
         def gather(window, offsets, dtype, name):
             picked = keep.tile([P, S], dtype, name=name, align_bytes=64)
@@ -73,6 +77,7 @@ def tile_list_altimeter_height_features_kernel(
         warm = keep.tile([P, 1], F32)
         nc.vector.memset(warm[:], 0.0)
         nc.scalar.activation(warm[:], warm[:], ACT.Silu)
+
         tab_sc = zeroed_scale_tile(2, T, "tab_sc")
         w1_sc = zeroed_scale_tile(2, H, "w1_sc")
         tab2_sc = zeroed_scale_tile(1, T3, "tab2_sc")
@@ -180,12 +185,11 @@ def tile_list_altimeter_height_features_kernel(
             rest_sb[s] = rest
 
         def take_tanh(s):
-            tanh_sb[s] = work.tile([P, S], F32, name="tanh_sb")
+            tanh_sb[s] = work.tile([P, S], F32, name="tanh_sb", tag="tanh%d" % (s % AHEAD), bufs=1)
             nc.scalar.activation(tanh_sb[s][:], tanh_acc[s][:], ACT.Tanh)
 
         def add_cos(s):
-            tag = "sea%d" % (s % 2) if s < SLICES - 1 else "factor%d" % (s - 1)
-            both = work.tile([P, S], F32, name="both", tag=tag, bufs=1)
+            both = work.tile([P, S], F32, name="both", tag="factor%d" % (s - 1) if s else "both", bufs=1)
             nc.scalar.activation(both[:], rest_sb[s][:], ACT.Sin, scale=-2.0 * math.pi)
             nc.vector.tensor_tensor(both[:], both[:], tanh_sb[s][:], ALU.add)
             both_sb[s] = both
@@ -194,17 +198,21 @@ def tile_list_altimeter_height_features_kernel(
             nc.vector.tensor_tensor(sea_pages[s // (SLICES - 1)][:].indirect(idx4[:]), both_sb[s][:], weights[s][:], ALU.mult)
 
         def place_echo(s):
-            h1 = work.tile([P, S], F32, name="h1", tag="factor%d" % (s - 2) if s >= 2 else "first%d" % s, bufs=1)
+            h1 = work.tile([P, S], F32, name="h1", tag="first%d" % s if s < AHEAD else "tanh%d" % (s % AHEAD), bufs=1)
             nc.scalar.copy(h1[:], echo_acc[s][:])
             nc.vector.tensor_tensor(echo_pages[s % ECHO_PAGES][:].indirect(idx3[:]), h1[:], wg1_sb[:], ALU.mult)
 
-        def turned_sum(banks, parts):
-            for n, part in enumerate(parts):
-                for block in range(T2 // P):
-                    half, i = divmod(block, 4)
-                    nc.tensor.matmul(banks[half][:, i * P : (i + 1) * P], lhsT=part[:, block * P : (block + 1) * P],
-                                     rhs=ident[:], start=(n == 0 and i == 0),
-                                     stop=(n == len(parts) - 1 and i == 3), is_transpose=True)
+        def turned_sum(banks, terms, held_back=None):
+            steps = [(n, block) for n in range(len(terms)) for block in range(T2 // P)]
+            if held_back is not None:
+                steps.remove(held_back)
+                steps.append(held_back)
+            for n, block in steps:
+                half, i = divmod(block, 4)
+                mine = [step for step in steps if step[1] // 4 == half]
+                nc.tensor.matmul(banks[half][:, i * P : (i + 1) * P], lhsT=terms[n][:, block * P : (block + 1) * P],
+                                 rhs=ident[:], start=((n, block) == mine[0]), stop=((n, block) == mine[-1]),
+                                 is_transpose=True)
 
         def by_word(acc):
             return acc[:].rearrange("m (i p u e) -> m u i p e", i=4, u=2, e=2)
@@ -229,14 +237,15 @@ def tile_list_altimeter_height_features_kernel(
         z_turned = {}
 
         def combine(s):
-            g, part = divmod(s, 4)
+            g, place = divmod(s, GROUP_SLICES)
             banks = [psum.tile([P, 512], F32, name="sum_acc%d" % half) for half in range(2)]
-            turned_sum(banks, [surf_sb[s], echo_pages[s % ECHO_PAGES], sea_pages[s // (SLICES - 1)]])
-            if part == 0:
+            turned_sum(banks, [surf_sb[s], echo_pages[s % ECHO_PAGES], sea_pages[s // (SLICES - 1)]],
+                       (1, T2 // P - 1) if s + ECHO_PAGES < SLICES else None)
+            if place == 0:
                 z_turned[g] = work.tile([P, 2, 4, 2, 4, 64], BF16, name="z_turned")
-            dst = z_turned[g][:, :, :, :, part, :].rearrange("m h i u (p e) -> m u h i p e", e=2)
+            dst = z_turned[g][:, :, :, :, place, :].rearrange("m h i u (p e) -> m u h i p e", e=2)
             if s < SLICES - 1:
-                rounded_sum = work.tile([P, 2, 2, 4, 32, 2], BF16, name="rounded_sum", tag="sea%d" % (s % 2), bufs=1)
+                rounded_sum = work.tile([P, 2, 2, 4, 32, 2], BF16, name="rounded_sum")
                 for half in range(2):
                     nc.scalar.copy(rounded_sum[:, :, half], by_word(banks[half]))
                 nc.vector.tensor_tensor(dst, rounded_sum[:], doubled[s][:], ALU.max)
@@ -269,9 +278,9 @@ def tile_list_altimeter_height_features_kernel(
             nc.sync.dma_start(raw[:], wz[512 * g : 512 * (g + 1), :].rearrange("(p j) n -> p j n", j=4))
             rounded = work.tile([P, 512, 4], BF16, name="rounded", align_bytes=64)
             for half in range(2):
-                part = slice(64 * half, 64 * (half + 1))
-                nc.scalar.copy(rounded[:].rearrange("p (t q) j -> p q t j", t=4)[:, part],
-                               raw[:].rearrange("p j (q t) -> p q t j", t=4)[:, part])
+                dealt = slice(64 * half, 64 * (half + 1))
+                nc.scalar.copy(rounded[:].rearrange("p (t f) j -> p f t j", t=4)[:, dealt],
+                               raw[:].rearrange("p j (f t) -> p f t j", t=4)[:, dealt])
             nc.vector.quantize_mx(out=wz_w[:, g, :].bitcast(E4M3), scales=wz_sc[:, g, :],
                                   in_=rounded[:].rearrange("p c j -> p (c j)"))
 
@@ -280,14 +289,14 @@ def tile_list_altimeter_height_features_kernel(
         def y_passes(c, bank, g):
             first, width = Y_CHUNKS[c]
             cols = slice(first, first + width)
-            rows = 512 // width
-            for e in range(rows):
-                t = rows * bank + e
+            per_bank = 512 // width
+            for e in range(per_bank):
+                t = per_bank * bank + e
                 nc.tensor.matmul_mx(
                     out=y_acc[c][bank][:, e * width : (e + 1) * width],
                     lhsT=wz_w[:, g, t * P : (t + 1) * P].bitcast(E4M3), lhsT_scale=wz_sc[:, g, t * P : (t + 1) * P],
                     rhs=z_w[g][:, cols].bitcast(E4M3), rhs_scale=z_sc[g][:, cols],
-                    start=(g == 0 and e == 0), stop=(g == GROUPS - 1 and e == rows - 1))
+                    start=(g == 0 and e == 0), stop=(g == GROUPS - 1 and e == per_bank - 1))
 
         def open_y(c):
             y_acc[c] = [psum.tile([P, 512], F32, name="y_acc", tag=tag) for tag in Y_BANKS[c]]
@@ -317,40 +326,43 @@ def tile_list_altimeter_height_features_kernel(
         double_q(0)
         sum_q(1)
         cos_product(2)
+        wa_left = WA_PARTS - len(wa_raw)
         for s in range(SLICES):
             place_sea(s)
-            if s + 2 < SLICES:
-                load_surf(s + 2)
-                place_echo(s + 2)
+            if s + AHEAD < SLICES:
+                load_surf(s + AHEAD)
+                place_echo(s + AHEAD)
             if s + 1 < SLICES:
                 add_cos(s + 1)
-            if s + 2 < SLICES:
-                reduce_angle(s + 2)
-                tanh_product(s + 2)
-            if s + 3 < SLICES:
-                cos_product(s + 3)
-                echo_product(s + 3)
+            if s + AHEAD < SLICES:
+                reduce_angle(s + AHEAD)
+                tanh_product(s + AHEAD)
+            if s + AHEAD + 1 < SLICES:
+                cos_product(s + AHEAD + 1)
+                echo_product(s + AHEAD + 1)
             if s == SLICES - 1:
                 open_y(1)
             combine(s)
             if s + 1 < SLICES:
                 double_q(s + 1)
-            if s + 2 < SLICES:
-                sum_q(s + 2)
-                take_tanh(s + 2)
-            if s in (0, 1):
-                load_wa(2 + s)
-                quantise_wa(2 + s)
-            if s in (2, 3):
-                quantise_wz(s - 2)
-            if s == 3:
+            if s + AHEAD < SLICES:
+                sum_q(s + AHEAD)
+                take_tanh(s + AHEAD)
+            if s < wa_left:
+                load_wa(WA_PARTS - wa_left + s)
+                quantise_wa(WA_PARTS - wa_left + s)
+            elif s < wa_left + GROUPS:
+                quantise_wz(s - wa_left)
+            if s == wa_left + GROUPS - 1:
                 for c, (first, width) in enumerate(Y_CHUNKS):
                     tile = keep.tile([P, 4, width], F32, name="y%d" % c)
                     nc.sync.dma_start(tile[:], resid_rows[:, :, first : first + width])
                     y_sb.append(tile)
-            for c, tag in EARLY_BACK.get(s, ()):
-                quantise_z(0, c, tag)
-            if s == 6:
+            first_chunk = BACK_PER_ROUND * (s - GROUP_SLICES)
+            if 0 <= first_chunk < CHUNKS:
+                for c in range(first_chunk, first_chunk + BACK_PER_ROUND):
+                    quantise_z(0, c, EARLY_BACK_BANKS[c])
+            if s == SLICES - AHEAD:
                 open_y(0)
 
         y_w = keep.tile([P, T2], U32, align_bytes=64)
@@ -360,16 +372,16 @@ def tile_list_altimeter_height_features_kernel(
         out_scales = out_2[0].bitcast(I32)
 
         for c in range(CHUNKS):
-            quantise_z(1, c, BACK_BANKS[c])
+            quantise_z(1, c, LATE_BACK_BANKS[c])
         for c, (first, width) in enumerate(Y_CHUNKS):
             cols = slice(first, first + width)
-            if c >= 2:
+            if c not in y_acc:
                 open_y(c)
             for bank, acc in enumerate(y_acc[c]):
                 y_passes(c, bank, 1)
-                count = 512 // width
-                rows = y_sb[c][:, count * bank : count * (bank + 1), :]
-                nc.vector.tensor_tensor(rows, acc[:].rearrange("p (e m) -> p e m", e=count), rows, ALU.add)
+                per_bank = 512 // width
+                y_part = y_sb[c][:, per_bank * bank : per_bank * (bank + 1), :]
+                nc.vector.tensor_tensor(y_part, acc[:].rearrange("p (e m) -> p e m", e=per_bank), y_part, ALU.add)
             nc.sync.dma_start(out_rows[:, :, cols], y_sb[c][:])
             y_in = work.tile([P, width, 4], BF16, name="y_in", bufs=3, align_bytes=64)
             rounding = nc.vector.tensor_copy if c == len(Y_CHUNKS) - 1 else nc.scalar.copy
@@ -379,6 +391,6 @@ def tile_list_altimeter_height_features_kernel(
             if first + width == T2 // 2:
                 nc.sync.dma_start(out_words[:, : T2 // 2], y_w[:, : T2 // 2].bitcast(I32))
         nc.scalar.dma_start(out_words[:, T2 // 2 :], y_w[:, T2 // 2 :].bitcast(I32))
-        for quad in range(4):
-            queue = nc.sync if quad < 2 else nc.scalar
-            queue.dma_start(out_scales[4 * quad : 4 * quad + 4, :], y_sc[32 * quad : 32 * quad + 4, :].bitcast(I32))
+        for d in range(4):
+            queue = nc.sync if d < 2 else nc.scalar
+            queue.dma_start(out_scales[4 * d : 4 * d + 4, :], y_sc[32 * d : 32 * d + 4, :].bitcast(I32))

import math
from contextlib import ExitStack

import concourse.mybir as mybir
from concourse.masks import make_identity

K, K2, T, T3, S, H, T2, N = 1024, 512, 2048, 1024, 512, 1024, 1024, 512
FLOPS = 2 * S * H * (K + 2 * K2) + 2 * H * N * T2

F32 = mybir.dt.float32
BF16 = mybir.dt.bfloat16
I32 = mybir.dt.int32
U32 = mybir.dt.uint32
U16 = mybir.dt.uint16
U8 = mybir.dt.uint8
E4M3 = mybir.dt.float8_e4m3fn_x4
E2M1 = mybir.dt.float4_e2m1fn_x4
ALU = mybir.AluOpType
ACT = mybir.ActivationFunctionType

P = 128
SLICES = H // P
GROUPS = H // 512
ROUNDER = 1.5 * 2.0**23
GROUP_SLICES = SLICES // GROUPS
AHEAD = 2
ECHO_PAGES = AHEAD + 1
SEA_PAGES = 2
WA_PART = 2 * P
WA_PARTS = H // WA_PART
CHUNK = 256
CHUNKS = T2 // CHUNK
BACK_PER_ROUND = 2
Y_CHUNKS = ((0, 256), (256, 256), (512, 256), (768, 128), (896, 128))
EARLY_BACK_BANKS = ("back_acc", "back_acc", "back_acc", "echo_acc")
LATE_BACK_BANKS = ("back_acc", "echo_acc", "sum_acc0", "back_acc")
Y_BANKS = (("cos_acc", "tanh_acc"), ("q_acc0", "q_acc1"), ("sum_acc1", "echo_acc"), ("sum_acc0",), ("back_acc",))


def tile_list_altimeter_height_features_kernel(
    tc, tab_words, tab_scales, tab2_words, tab2_scales, offs, offs2, offs3, offs4,
    w1_words, w1_scales, wa, wb_words, wb_scales, gain, wg1, wg2, surf, wz, resid,
    out_0, out_1, out_2,
):
    nc = tc.nc
    with ExitStack() as ctx:
        lists = ctx.enter_context(tc.tile_pool(name="lists", bufs=1))
        keep = ctx.enter_context(tc.tile_pool(name="keep", bufs=1))
        work = ctx.enter_context(tc.tile_pool(name="work", bufs=2))
        psum = ctx.enter_context(tc.psum_pool(name="psum", bufs=1))

        def load_list(src, name):
            tile = lists.tile([P, S // 16], U16, name=name)
            nc.sync.dma_start(tile[:], src)
            return tile

        def load_words(src, width, name):
            tile = keep.tile([P, width], I32, name=name, align_bytes=64)
            nc.sync.dma_start(tile[:], src.bitcast(I32))
            return tile

        def zeroed_scale_tile(passes, width, name):
            tile = keep.tile([P, passes, width // 4], I32, name=name, align_bytes=64)
            nc.vector.memset(tile[:], 0)
            return tile

        def load_scale_rows(tile, src):
            by_row = src.bitcast(I32).rearrange("a (d i) c -> i d a c", i=4)
            for i in range(4):
                nc.sync.dma_start(tile[i:P:32], by_row[i])

        def gather(window, offsets, dtype, name):
            picked = keep.tile([P, S], dtype, name=name, align_bytes=64)
            nc.vector.tensor_copy(picked[:], window.bitcast(dtype).indirect(offsets[:]))
            return picked

        warm = keep.tile([P, 1], F32)
        nc.vector.memset(warm[:], 0.0)
        nc.scalar.activation(warm[:], warm[:], ACT.Silu)

        tab_sc = zeroed_scale_tile(2, T, "tab_sc")
        w1_sc = zeroed_scale_tile(2, H, "w1_sc")
        tab2_sc = zeroed_scale_tile(1, T3, "tab2_sc")
        wb_sc = zeroed_scale_tile(1, H, "wb_sc")

        gain_rows = keep.tile([P, P], F32)
        nc.gpsimd.memset(gain_rows[:], 0.0)
        ident = keep.tile([P, P], F32)
        make_identity(nc, ident[:])
        idx = load_list(offs, "idx")
        tab_w = [load_words(tab_words[0].rearrange("p t i -> p (t i)"), T, "tab_w0")]
        load_scale_rows(tab_sc, tab_scales)
        nc.sync.dma_start(gain_rows[:SLICES, :], gain.rearrange("(s p) -> s p", p=P))
        wg2_sb = keep.tile([P, S], F32)
        nc.sync.dma_start(wg2_sb[:], wg2)
        gain_acc = psum.tile([P, 512], F32, name="gain_acc", tag="back_acc")
        nc.tensor.transpose(gain_acc[:, :P], gain_rows[:], ident[:])
        gain_sb = keep.tile([P, SLICES], F32)
        nc.scalar.copy(gain_sb[:], gain_acc[:, :SLICES])
        weights = []
        for s in range(SLICES):
            weight = work.tile([P, S], F32, name="weight", tag="factor%d" % s, bufs=1)
            nc.scalar.activation(weight[:], wg2_sb[:], ACT.Copy, scale=gain_sb[:, s : s + 1])
            weights.append(weight)
        tab_w.append(load_words(tab_words[1].rearrange("p t i -> p (t i)"), T, "tab_w1"))
        w1_w = keep.tile([P, 2, H // 2], I32, align_bytes=64)
        nc.sync.dma_start(w1_w[:], w1_words.bitcast(I32).rearrange("a p c -> p a c"))
        load_scale_rows(w1_sc, w1_scales)
        idx2 = load_list(offs2, "idx2")
        tab2_w = load_words(tab2_words[0].rearrange("p t i -> p (t i)"), T3, "tab2_w")
        load_scale_rows(tab2_sc, tab2_scales)
        idx3 = load_list(offs3, "idx3")
        wg1_sb = keep.tile([P, S], F32)
        nc.sync.dma_start(wg1_sb[:], wg1)

        def zeroed_page(name):
            page = keep.tile([P, T2], F32, name=name)
            nc.gpsimd.memset(page[:], 0.0)
            return page

        echo_pages = [zeroed_page("echo_page%d" % i) for i in range(ECHO_PAGES)]
        sea_pages = [zeroed_page("sea_page%d" % i) for i in range(SEA_PAGES)]

        surf_sb = {}

        def load_surf(s):
            tile = work.tile([P, T2], F32, name="surf_rows", bufs=ECHO_PAGES + 1)
            nc.sync.dma_start(tile[:], surf[s * P : (s + 1) * P, :])
            surf_sb[s] = tile

        wa_raw = []

        def load_wa(part):
            raw = work.tile([P, 4, WA_PART], F32, name="wa_raw")
            nc.sync.dma_start(raw[:], wa[:, WA_PART * part : WA_PART * (part + 1)].rearrange("(p j) c -> p j c", j=4))
            wa_raw.append(raw)

        wb_w = load_words(wb_words[0].rearrange("p c i -> p (c i)"), H, "wb_w")
        load_scale_rows(wb_sc, wb_scales)
        idx4 = load_list(offs4, "idx4")
        load_wa(0)
        load_surf(0)
        load_wa(1)
        load_surf(1)

        v_w = [gather(tab_w[0][:], idx, U32, "v_w0")]
        v_sc = [gather(tab_sc[:, a, :], idx, U8, "v_sc%d" % a) for a in range(2)]
        v_w.append(gather(tab_w[1][:], idx, U32, "v_w1"))
        v2_w = gather(tab2_w[:], idx2, U32, "v2_w")
        v2_sc = gather(tab2_sc[:, 0, :], idx2, U8, "v2_sc")

        wa_w = keep.tile([P, H], U32, align_bytes=64)
        wa_sc = keep.tile([P, H], U8, align_bytes=64)
        echo_acc, cos_acc, tanh_acc, rest_sb, tanh_sb, both_sb, q_acc, doubled = {}, {}, {}, {}, {}, {}, {}, {}

        def sea_product(s, words, scales, name):
            cols = slice(s * P, (s + 1) * P)
            acc = psum.tile([P, S], F32, name=name)
            nc.tensor.matmul_mx(out=acc[:], lhsT=words[:, cols].bitcast(E4M3), lhsT_scale=scales[:, cols],
                                rhs=v2_w[:].bitcast(E4M3), rhs_scale=v2_sc[:], start=True, stop=True)
            return acc

        def echo_product(s):
            acc = psum.tile([P, S], F32, name="echo_acc")
            for a in range(2):
                nc.tensor.matmul_mx(
                    out=acc[:], lhsT=w1_w[:, a, :].bitcast(U8)[:, 2 * s * P : 2 * (s + 1) * P].bitcast(E2M1),
                    lhsT_scale=w1_sc[:, a, :].bitcast(U8)[:, s * P : (s + 1) * P],
                    rhs=v_w[a][:].bitcast(E4M3), rhs_scale=v_sc[a][:], start=(a == 0), stop=(a == 1))
            echo_acc[s] = acc

        def cos_product(s):
            cos_acc[s] = sea_product(s, wb_w, wb_sc[:, 0, :].bitcast(U8), "cos_acc")

        def tanh_product(s):
            tanh_acc[s] = sea_product(s, wa_w, wa_sc, "tanh_acc")

        def reduce_angle(s):
            tag, bufs = ("first1", 1) if s == 0 else ("turns", 2)
            turns = work.tile([P, S], F32, name="turns", tag=tag, bufs=bufs)
            nc.scalar.activation(turns[:], cos_acc[s][:], ACT.Copy, bias=0.25, scale=1.0 / (2.0 * math.pi))
            rest = work.tile([P, S], F32, bufs=1)
            nc.scalar.activation(rest[:], turns[:], ACT.Copy, bias=ROUNDER, scale=1.0)
            nc.vector.scalar_tensor_tensor(rest[:], rest[:], ROUNDER, turns[:], ALU.subtract, ALU.subtract)
            rest_sb[s] = rest

        def take_tanh(s):
            tanh_sb[s] = work.tile([P, S], F32, name="tanh_sb", tag="tanh%d" % (s % AHEAD), bufs=1)
            nc.scalar.activation(tanh_sb[s][:], tanh_acc[s][:], ACT.Tanh)

        def add_cos(s):
            both = work.tile([P, S], F32, name="both", tag="factor%d" % (s - 1) if s else "both", bufs=1)
            nc.scalar.activation(both[:], rest_sb[s][:], ACT.Sin, scale=-2.0 * math.pi)
            nc.vector.tensor_tensor(both[:], both[:], tanh_sb[s][:], ALU.add)
            both_sb[s] = both

        def place_sea(s):
            nc.vector.tensor_tensor(sea_pages[s // (SLICES - 1)][:].indirect(idx4[:]), both_sb[s][:], weights[s][:], ALU.mult)

        def place_echo(s):
            h1 = work.tile([P, S], F32, name="h1", tag="first%d" % s if s < AHEAD else "tanh%d" % (s % AHEAD), bufs=1)
            nc.scalar.copy(h1[:], echo_acc[s][:])
            nc.vector.tensor_tensor(echo_pages[s % ECHO_PAGES][:].indirect(idx3[:]), h1[:], wg1_sb[:], ALU.mult)

        def turned_sum(banks, terms, held_back=None):
            steps = [(n, block) for n in range(len(terms)) for block in range(T2 // P)]
            if held_back is not None:
                steps.remove(held_back)
                steps.append(held_back)
            for n, block in steps:
                half, i = divmod(block, 4)
                mine = [step for step in steps if step[1] // 4 == half]
                nc.tensor.matmul(banks[half][:, i * P : (i + 1) * P], lhsT=terms[n][:, block * P : (block + 1) * P],
                                 rhs=ident[:], start=((n, block) == mine[0]), stop=((n, block) == mine[-1]),
                                 is_transpose=True)

        def by_word(acc):
            return acc[:].rearrange("m (i p u e) -> m u i p e", i=4, u=2, e=2)

        def sum_q(s):
            q_acc[s] = [psum.tile([P, 512], F32, name="q_acc%d" % half) for half in range(2)]
            turned_sum(q_acc[s], [surf_sb[s], echo_pages[s % ECHO_PAGES]])

        def double_q(s):
            doubled[s] = work.tile([P, 2, 2, 4, 32, 2], BF16, name="twice_q", bufs=4)
            for half in range(2):
                nc.scalar.activation(doubled[s][:, :, half], by_word(q_acc[s][half]), ACT.Copy, scale=2.0)

        def quantise_wa(part):
            cols = slice(WA_PART * part, WA_PART * (part + 1))
            rounded = work.tile([P, WA_PART, 4], BF16, name="rounded", align_bytes=64)
            nc.scalar.copy(rounded[:].rearrange("p (c i) j -> p c j i", i=4),
                           wa_raw[part][:].rearrange("p j (c i) -> p c j i", i=4))
            nc.vector.quantize_mx(out=wa_w[:, cols].bitcast(E4M3), scales=wa_sc[:, cols],
                                  in_=rounded[:].rearrange("p c j -> p (c j)"))

        z_turned = {}

        def combine(s):
            g, place = divmod(s, GROUP_SLICES)
            banks = [psum.tile([P, 512], F32, name="sum_acc%d" % half) for half in range(2)]
            turned_sum(banks, [surf_sb[s], echo_pages[s % ECHO_PAGES], sea_pages[s // (SLICES - 1)]],
                       (1, T2 // P - 1) if s + ECHO_PAGES < SLICES else None)
            if place == 0:
                z_turned[g] = work.tile([P, 2, 4, 2, 4, 64], BF16, name="z_turned")
            dst = z_turned[g][:, :, :, :, place, :].rearrange("m h i u (p e) -> m u h i p e", e=2)
            if s < SLICES - 1:
                rounded_sum = work.tile([P, 2, 2, 4, 32, 2], BF16, name="rounded_sum")
                for half in range(2):
                    nc.scalar.copy(rounded_sum[:, :, half], by_word(banks[half]))
                nc.vector.tensor_tensor(dst, rounded_sum[:], doubled[s][:], ALU.max)
            else:
                for half in range(2):
                    nc.vector.tensor_tensor(dst[:, :, half], by_word(banks[half]), doubled[s][:, :, half], ALU.max)

        z_w = [keep.tile([P, T2], U32, name="z_w%d" % g, align_bytes=64) for g in range(GROUPS)]
        z_sc = [keep.tile([P, T2], U8, name="z_sc%d" % g, align_bytes=64) for g in range(GROUPS)]

        def quantise_z(g, c, tag):
            words = z_turned[g][:, c // 2].rearrange("m i u s x -> m (i u s x)").bitcast(F32)
            acc = psum.tile([P, 512], F32, name="back_acc", tag=tag)
            for i in range(2):
                for u in range(2):
                    block = 2 * (2 * (c % 2) + i) + u
                    nc.tensor.transpose(acc[:, u * CHUNK + i * P : u * CHUNK + (i + 1) * P],
                                        words[:, block * P : (block + 1) * P], ident[:])
            z_in = work.tile([P, CHUNK, 2], F32, name="z_in", bufs=3, align_bytes=64)
            nc.scalar.copy(z_in[:], acc[:].rearrange("p (u m) -> p m u", u=2))
            cols = slice(c * CHUNK, (c + 1) * CHUNK)
            nc.vector.quantize_mx(out=z_w[g][:, cols].bitcast(E4M3), scales=z_sc[g][:, cols],
                                  in_=z_in[:].rearrange("p m u -> p (m u)").bitcast(BF16))

        wz_w = keep.tile([P, GROUPS, N], U32, align_bytes=64)
        wz_sc = keep.tile([P, GROUPS, N], U8, align_bytes=64)

        def quantise_wz(g):
            raw = work.tile([P, 4, N], F32, name="raw")
            nc.sync.dma_start(raw[:], wz[512 * g : 512 * (g + 1), :].rearrange("(p j) n -> p j n", j=4))
            rounded = work.tile([P, 512, 4], BF16, name="rounded", align_bytes=64)
            for half in range(2):
                dealt = slice(64 * half, 64 * (half + 1))
                nc.scalar.copy(rounded[:].rearrange("p (t f) j -> p f t j", t=4)[:, dealt],
                               raw[:].rearrange("p j (f t) -> p f t j", t=4)[:, dealt])
            nc.vector.quantize_mx(out=wz_w[:, g, :].bitcast(E4M3), scales=wz_sc[:, g, :],
                                  in_=rounded[:].rearrange("p c j -> p (c j)"))

        y_acc = {}

        def y_passes(c, bank, g):
            first, width = Y_CHUNKS[c]
            cols = slice(first, first + width)
            per_bank = 512 // width
            for e in range(per_bank):
                t = per_bank * bank + e
                nc.tensor.matmul_mx(
                    out=y_acc[c][bank][:, e * width : (e + 1) * width],
                    lhsT=wz_w[:, g, t * P : (t + 1) * P].bitcast(E4M3), lhsT_scale=wz_sc[:, g, t * P : (t + 1) * P],
                    rhs=z_w[g][:, cols].bitcast(E4M3), rhs_scale=z_sc[g][:, cols],
                    start=(g == 0 and e == 0), stop=(g == GROUPS - 1 and e == per_bank - 1))

        def open_y(c):
            y_acc[c] = [psum.tile([P, 512], F32, name="y_acc", tag=tag) for tag in Y_BANKS[c]]
            for bank in range(len(y_acc[c])):
                y_passes(c, bank, 0)

        y_sb = []
        resid_rows = resid.rearrange("(p t) m -> p t m", t=4)

        echo_product(0)
        place_echo(0)
        echo_product(1)
        cos_product(0)
        reduce_angle(0)
        quantise_wa(0)
        place_echo(1)
        echo_product(2)
        tanh_product(0)
        take_tanh(0)
        add_cos(0)
        cos_product(1)
        reduce_angle(1)
        tanh_product(1)
        take_tanh(1)
        quantise_wa(1)
        sum_q(0)
        double_q(0)
        sum_q(1)
        cos_product(2)
        wa_left = WA_PARTS - len(wa_raw)
        for s in range(SLICES):
            place_sea(s)
            if s + AHEAD < SLICES:
                load_surf(s + AHEAD)
                place_echo(s + AHEAD)
            if s + 1 < SLICES:
                add_cos(s + 1)
            if s + AHEAD < SLICES:
                reduce_angle(s + AHEAD)
                tanh_product(s + AHEAD)
            if s + AHEAD + 1 < SLICES:
                cos_product(s + AHEAD + 1)
                echo_product(s + AHEAD + 1)
            if s == SLICES - 1:
                open_y(1)
            combine(s)
            if s + 1 < SLICES:
                double_q(s + 1)
            if s + AHEAD < SLICES:
                sum_q(s + AHEAD)
                take_tanh(s + AHEAD)
            if s < wa_left:
                load_wa(WA_PARTS - wa_left + s)
                quantise_wa(WA_PARTS - wa_left + s)
            elif s < wa_left + GROUPS:
                quantise_wz(s - wa_left)
            if s == wa_left + GROUPS - 1:
                for c, (first, width) in enumerate(Y_CHUNKS):
                    tile = keep.tile([P, 4, width], F32, name="y%d" % c)
                    nc.sync.dma_start(tile[:], resid_rows[:, :, first : first + width])
                    y_sb.append(tile)
            first_chunk = BACK_PER_ROUND * (s - GROUP_SLICES)
            if 0 <= first_chunk < CHUNKS:
                for c in range(first_chunk, first_chunk + BACK_PER_ROUND):
                    quantise_z(0, c, EARLY_BACK_BANKS[c])
            if s == SLICES - AHEAD:
                open_y(0)

        y_w = keep.tile([P, T2], U32, align_bytes=64)
        y_sc = keep.tile([P, T2], U8, align_bytes=64)
        out_rows = out_0.rearrange("(p t) m -> p t m", t=4)
        out_words = out_1[0].rearrange("p m t -> p (m t)").bitcast(I32)
        out_scales = out_2[0].bitcast(I32)

        for c in range(CHUNKS):
            quantise_z(1, c, LATE_BACK_BANKS[c])
        for c, (first, width) in enumerate(Y_CHUNKS):
            cols = slice(first, first + width)
            if c not in y_acc:
                open_y(c)
            for bank, acc in enumerate(y_acc[c]):
                y_passes(c, bank, 1)
                per_bank = 512 // width
                y_part = y_sb[c][:, per_bank * bank : per_bank * (bank + 1), :]
                nc.vector.tensor_tensor(y_part, acc[:].rearrange("p (e m) -> p e m", e=per_bank), y_part, ALU.add)
            nc.sync.dma_start(out_rows[:, :, cols], y_sb[c][:])
            y_in = work.tile([P, width, 4], BF16, name="y_in", bufs=3, align_bytes=64)
            rounding = nc.vector.tensor_copy if c == len(Y_CHUNKS) - 1 else nc.scalar.copy
            rounding(y_in[:].rearrange("p (c i) t -> p c t i", i=4), y_sb[c][:].rearrange("p t (c i) -> p c t i", i=4))
            nc.vector.quantize_mx(out=y_w[:, cols].bitcast(E4M3), scales=y_sc[:, cols],
                                  in_=y_in[:].rearrange("p m t -> p (m t)"))
            if first + width == T2 // 2:
                nc.sync.dma_start(out_words[:, : T2 // 2], y_w[:, : T2 // 2].bitcast(I32))
        nc.scalar.dma_start(out_words[:, T2 // 2 :], y_w[:, T2 // 2 :].bitcast(I32))
        for d in range(4):
            queue = nc.sync if d < 2 else nc.scalar
            queue.dma_start(out_scales[4 * d : 4 * d + 4, :], y_sc[32 * d : 32 * d + 4, :].bitcast(I32))
